import numpy as np, ml_dtypes
CORES = [1,5,17,21,33,37,49,53]
N = 8
import mx_ref
BF = ml_dtypes.bfloat16
def gentries(a):
    return np.ascontiguousarray(a.reshape(8, 16, -1).transpose(0, 2, 1)).reshape(8, -1)
def gtable(e):
    e = np.asarray(e); return np.ascontiguousarray(e.reshape(8, -1, 16).transpose(0, 2, 1)).reshape(128, -1).astype(np.int32)
def tile(rs):
    return np.stack(rs, axis=2).reshape(128, -1).astype(BF)
def pick(q, e):
    c = np.concatenate([q[0].reshape(128, -1, 4), np.zeros((128, 1, 4), np.uint8)], axis=1); s = np.concatenate([q[1], np.ones((16, 1), np.uint8)], axis=1)
    return (np.ascontiguousarray(c[:, e].reshape(128, -1)), np.ascontiguousarray(s[:, e]))
def join(*qs):
    return (np.concatenate([q[0] for q in qs], axis=1), np.concatenate([q[1] for q in qs], axis=1))
def put(q, e, v):
    c, s = q[0].reshape(128, -1, 4).copy(), q[1].copy(); c[:, e] = v[0].reshape(128, -1, 4); s[:, e] = v[1]
    return (c.reshape(128, -1), s)
def pk(c, s):
    return (np.ascontiguousarray(c), mx_ref.live(s))
def emit(q):
    return q[0], q[1]
def packed(v, rng):
    q = [mx_ref.quantize(np.ascontiguousarray(v[r])) for r in range(N)]
    return np.stack([a for a, b in q]), np.stack([mx_ref.plane(b, rng) for a, b in q])
def values_of_codes():
    e, c = np.zeros((128, 128, 4), np.float32), np.zeros((128, 2, 4), np.uint8)
    e[np.arange(128), np.arange(128), 0] = 1
    c[:127, :, 0] = np.arange(256).reshape(2, 128).T[:127]
    return mx_ref.matmul(mx_ref.quantize(e.reshape(128, 512).astype(BF)), (c.reshape(128, 8), np.full((16, 2), 127, np.uint8))).T.reshape(-1).astype(np.float64)
CODE_VALUE, SCALE_VALUE = values_of_codes(), 2.0 ** (np.arange(256) - 127.0)
def decode(q):
    return (CODE_VALUE[q[0]].reshape(16, 8, -1, 4) * SCALE_VALUE[q[1]][:, None, :, None] + 0.0).reshape(128, -1).astype(np.float32)
def f(rng, *shape):
    return mx_ref.flush((rng.standard_normal(shape, dtype=np.float32) * np.exp2(rng.integers(-2, 3, shape[:-1] + (1,)))).astype(BF))
def wide(rng, *shape, cols=0):
    v = rng.standard_normal(shape, dtype=np.float32) * np.exp2(rng.integers(-12, 13, shape)).astype(np.float32)
    if cols: v *= np.repeat(np.exp2(rng.integers(-cols, cols + 1, shape[:-2] + (1, shape[-1] // 4))) * (rng.random(shape[:-2] + (1, shape[-1] // 4)) > 0.0625), 4, axis=-1).astype(np.float32)
    return mx_ref.flush(v.astype(BF))
C, B, L, M, R = 256, 32, 320, 128, 3
MASK = [1, 2, 4]
def big(v):
    v = v.astype(np.float32)
    v[np.abs(v) < np.float32(2.0 ** -16)] = 0
    return v.astype(BF)
def numbers_of(rng):
    return {"x": big(f(rng, N, 128, 4 * C)), "u": np.array(f(rng, N, 128, 512)), "v": np.array(f(rng, N, 128, 512))}
def rings(rng, ends=False):
    p = [np.arange(C)[::1 - 2 * (h % 2)] if ends else rng.permutation(C) for h in range(8)]
    e = np.zeros((8, L), np.int64)
    for g in range(8):
        a, b = (g - 1) % 8, (g + 1) % 8
        e[g] = rng.permutation(np.concatenate([C * g + np.arange(C), C * a + p[a][:B], C * b + p[b][B:2 * B]]))
        if ends: e[g] = np.sort(e[g])[::1 - 2 * (g // 2 % 2)]
    return np.stack([gtable(e)] * N)
def layers(rng):
    return big(np.clip(f(rng, N, 128, 2048).astype(np.float32) * np.float32(0.25), -1.75, 1.75)).reshape(N, 8, 16, 4, 8, 16, 4)
def weights(rng, w):
    c, s = packed(np.ascontiguousarray(w).reshape(N, 128, 2048), rng)
    return {"wc": c, "ws": s}
def setup_inputs(rng):
    return {**numbers_of(rng), "ring": rings(rng), **weights(rng, layers(rng))}
def setup_inputs_ties(rng):
    d = numbers_of(rng)
    o = rng.permutation(N)
    same = rng.random((N, 8, C)) < rng.random((N, 8, 1))
    same[o[0]] = True
    same[o[0], rng.integers(8)] = False
    a = rng.integers(0, 3, (N, 8, C))
    b = np.where(same, a, rng.integers(0, 3, (N, 8, C)))
    least = max(257 if C > 256 else 0, 17 * C // 20) | 1
    for r in o[1:]:
        n = rng.permutation(np.arange(least, 19 * C // 20 + 1, 2))[:3]
        for i, g in enumerate(rng.permutation(8)[:3]):
            b[r, g] = a[r, g]
            j = rng.permutation(C)[:n[i]]
            more = rng.integers(1, 3, n[i])
            less = rng.integers(0, more)
            a[r, g, j] = more if o[r] % 2 else less
            b[r, g, j] = less if o[r] % 2 else more
    x = d["x"].reshape(N, 8, 16, C, 4)
    x[:, :, 0] = 0
    x[:, :, 0, :, 0] = a.astype(np.float32).astype(BF)
    x[:, :, 0, :, 1] = b.astype(np.float32).astype(BF)
    u = d["u"].reshape(N, 128, 128, 4)
    u[:, :, ::16] = 0
    for r in range(N):
        for h in range(0, 128, 16):
            u[r, h, h, 0] = 1.0 if o[r] % 2 else -1.0
            u[r, h, h, 1] = -1.0 if o[r] % 2 else 1.0
    w = layers(rng)
    w[:, :, :, :, :, 0] = 0
    return {"x": x.reshape(N, 128, 4 * C), "u": u.reshape(N, 128, 512), "v": d["v"], "ring": rings(rng), **weights(rng, w)}
def setup_inputs_near(rng):
    d = numbers_of(rng)
    o = rng.permutation(N) % 4
    k = rng.integers(0, 4, (N, 8, C))
    a = np.array([1.125, -1.125, 1.0, -1.0])[k]
    b = np.array([-1.25, 1.25, -1.125, 1.125])[k]
    x = d["x"].astype(np.float32).reshape(N, 8, 16, C, 4)
    x[:, :, :8] = 0
    u = d["u"].reshape(N, 128, 128, 4)
    u[:, :, ::16] = 0
    i = np.arange(32)
    s = np.exp2(-12.0 - i // 2 % 4)
    for r in range(N):
        z = 2.0 ** -30 if o[r] < 2 else 1.0
        x[r, :, 0, :, 0] = a[r] * z
        x[r, :, 1, :, 0] = b[r] * z
        for g in range(8):
            j = rng.permutation(C)[:32]
            x[r, g, 0, j, 0] = 0
            x[r, g, 1, j, 0] = 0
            x[r, g, 2, j, 0] = 1.96875
            x[r, g, 3, j, 0] = np.where(i % 2 == 0, 1.5, 1.125) * s
            x[r, g, 4, j, 0] = np.where(i % 2 == 0, -1.375, -1.0) * s
        for g in rng.permutation(8)[:4]:
            j = rng.integers(C)
            x[r, g, :8, j] = 0
            x[r, g, 0, j, 0] = 2.0 ** 14 * rng.choice([-1.0, 1.0])
        for h in range(0, 128, 16):
            z = 2.0 ** -30 if o[r] % 2 == 0 else 1.0
            u[r, h, h, 0] = 1.125 * z
            u[r, h + 1, h, 0] = z
            u[r, h + 3, h, 0] = z
            u[r, h + 4, h, 0] = z
    w = layers(rng)
    w[:, :, :8] = 0
    w[:, :, :, :, :, :8] = 0
    for g in range(8): w[:, g, 2, 0, g, 2, 0] = -0.5
    return {"x": x.reshape(N, 128, 4 * C).astype(BF), "u": u.reshape(N, 128, 512), "v": d["v"], "ring": rings(rng), **weights(rng, w)}
def setup_inputs_late(rng):
    d = numbers_of(rng)
    x = d["x"].astype(np.float32).reshape(N, 8, 16, C, 4)
    x[:, :, 0] = ((rng.permutation(N) % 2) * 0.25 - 0.125)[:, None, None, None]
    s = (N, 8, 8, C, 4)
    x[:, :, 8:] = rng.choice([-1.0, 1.0], s) * (1.0 + 0.125 * (2 * rng.integers(0, 4, s) + 1)) * np.exp2(10.0 - rng.integers(8, 15, s))
    x[:, :, 8, :, 0] = rng.choice([-1.0, 1.0], (N, 8, C)) * 1.96875 * 2.0 ** 10
    u = d["u"].reshape(N, 128, 128, 4)
    u[:, :, ::16] = 0
    for h in range(0, 128, 16): u[:, h, h, 0] = 1.0
    w = layers(rng)
    w[:, :, 8] = 0
    w[:, :, :, :, :, 8:] = (w[:, :, :, :, :, 8:].astype(np.float32) * np.float32(0.125)).astype(BF)
    w[:, :, :, 0, :, 8] = 0
    for g in range(8): w[:, g, 8, 0, g, 8, 0] = -0.5
    return {"x": x.reshape(N, 128, 4 * C).astype(BF), "u": u.reshape(N, 128, 512), "v": d["v"], "ring": rings(rng), **weights(rng, w)}
def setup_inputs_ends(rng):
    d = numbers_of(rng)
    o = rng.permutation(N)
    x = np.zeros((N, 8, 16, C, 4), np.float32)
    u = d["u"].reshape(N, 128, 128, 4)
    u[:, :, ::16] = 0
    v = rng.choice([-1.0, 1.0], (N, 128, 512)).astype(np.float32)
    w = np.zeros((N, 8, 16, 4, 8, 16, 4), np.float32)
    for r in range(N):
        i = o[r] % 4
        k = np.array([1.0, 1.0, 1.0, -1.0, -1.0, -1.0, 0.0, 0.0])[rng.permutation(8)]
        x[r, :, :8] = k[:, None, None, None] * (2.0 ** 14 if i % 2 == 0 else 2.0 ** -30)
        x[r, :, 8:] = 2.0 ** 14 * rng.choice([-1.0, 1.0], (1, 1, C, 1) if i < 2 else (8, 8, C, 4))
        z = 2.0 ** 30 if i // 2 == 0 else 2.0 ** -30
        s = rng.choice([-1.0, 1.0])
        for h in range(0, 128, 16): u[r, h:h + 8, h] = s * z
        v[r] *= np.float32(z)
        w[r, :, 8:, :, :, 8:] = 1.96875 if i == 0 else -1.96875 if i == 3 else (1.96875 if i == 1 else 2.0 ** -30) * rng.choice([-1.0, 1.0], (8, 8, 4, 8, 8, 4))
    return {"x": x.reshape(N, 128, 4 * C).astype(BF), "u": u.reshape(N, 128, 512), "v": v.astype(BF), "ring": rings(rng, True), **weights(rng, w.astype(BF))}
def setup_inputs_spread(rng):
    d = setup_inputs(rng)
    d["x"] = big(wide(rng, N, 128, 4 * C, cols=3).astype(np.float32) * np.float32(0.03125))
    return d
def check_inputs(d):
    b = []
    for k, most in (("x", 2.0 ** 14), ("u", 2.0 ** 30), ("v", 2.0 ** 30)):
        a = np.abs(d[k].astype(np.float32))
        if not (np.isfinite(a).all() and ((a == 0) | (a >= 2.0 ** -30) & (a <= most)).all()): b.append("a value of " + k)
    if (d["ring"] != d["ring"][:1]).any(): b.append("ring isn't the same on all ranks")
    e = gentries(d["ring"][0])
    if not ((e >= 0) & (e < 8 * C)).all(): b.append("an entry of ring")
    for g in range(8):
        h = e[g] // C
        if np.unique(e[g]).size != L: b.append("a place twice in a ring")
        if np.count_nonzero(h == g) != C or np.count_nonzero(h == (g - 1) % 8) != B or np.count_nonzero(h == (g + 1) % 8) != B: b.append("the groups of a ring's places")
    for k in range(2):
        if np.unique(e[k::2]).size != 4 * L: b.append("rings of equal parity share a place")
    none, least, most = [emit(mx_ref.quantize(np.full((128, 16), k, np.float32).astype(BF)))[1][0, 0] for k in (0.0, 2.0 ** -30, 1.96875)]
    for r in range(N):
        if ((d["wc"][r] == 0x7F) | (d["wc"][r] == 0xFF)).any(): b.append("wc: a code that is no number")
        s = mx_ref.live(d["ws"][r])
        if ((s != none) & ((s < least) | (s > most))).any(): b.append("ws: a scale out of range")
        elif (np.abs(decode(pk(d["wc"][r], d["ws"][r]))) > 2.0).any(): b.append("a number of W beyond 2 in size")
    return b
def turned(e, a):
    now = np.arange(8 * C)
    for first in (1, 0):
        new = now.copy()
        for g in range(first, 8, 2): new[np.roll(e[g], -a[g])] = now[e[g]]
        now = new
    return now.reshape(8, C)
def reference(x, u, v, ring, wc, ws):
    qu = [mx_ref.quantize(u[r]) for r in range(N)]
    lay = [pk(wc[r], ws[r]) for r in range(N)]
    now = [x[r] for r in range(N)]
    e = gentries(ring[0])
    ac = np.zeros((N, 8, R), np.float32)
    for t in range(R):
        own, sent = [], []
        for r in range(N):
            q = mx_ref.quantize(now[r])
            s = mx_ref.matmul(qu[r], q)
            a = np.count_nonzero(s[::16] > 0, axis=1)
            ac[r, :, t] = a
            p = turned(e, a)
            own.append(np.ascontiguousarray(decode(q).reshape(8, 16, C, 4)[p // C, :, p % C].transpose(0, 2, 1, 3)).reshape(128, 4 * C).astype(BF))
            sent.append(decode(mx_ref.quantize(np.ascontiguousarray(own[r][:, :4 * M]))).astype(BF))
        for r in range(N):
            z = np.concatenate([sent[r ^ MASK[t]], own[r][:, 4 * M:]], axis=1)
            q = mx_ref.quantize(z)
            now[r] = tile([mx_ref.matmul(pick(lay[r], np.arange(128 * b, 128 * b + 128)), q) * np.float32(0.03125) + z[:, b::4].astype(np.float32) for b in range(4)])
    y = np.zeros((N, 128, C), np.float32)
    oc, osc = np.zeros((N, 128, 4 * C), np.uint8), np.zeros((N, 16, C), np.uint8)
    for r in range(N):
        q = mx_ref.quantize(now[r])
        y[r] = mx_ref.matmul(mx_ref.quantize(v[r]), q)
        oc[r], osc[r] = emit(q)
    return {"y": y, "ac": ac, "oc": oc, "osc": osc}

@@ -1,0 +1,440 @@
+from concourse.mybir import dt, AluOpType as A, ActivationFunctionType as F
+
+MASKS = [1, 2, 4]
+NV_FIRST, NV_LATE, NV_EARLY = 2, 6, 14
+NV_R0 = 6
+NS_TABLES = 10
+
+F32, BF, I32, U16, U8, MXW = "float32", "bfloat16", "int32", "uint16", "uint8", "float8_e4m3fn_x4"
+
+
+def _sb(n, d):
+    return ("sbuf", [128, n], d)
+
+
+SCRATCH = {
+    "ps": ("psum", [128, 4096], F32),
+    "xb": _sb(1024, BF), "ub": _sb(512, BF), "vb": _sb(512, BF), "rl": _sb(120, I32),
+    "uq": _sb(128, MXW), "us": _sb(128, U8), "uq2": _sb(128, MXW), "us2": _sb(128, U8),
+    "vq": _sb(128, MXW), "vs": _sb(128, U8), "wq": _sb(512, MXW), "wp": _sb(512, U8),
+    "et": _sb(1668, BF), "it": _sb(1028, BF), "ot": _sb(512, BF), "bt": _sb(512, BF),
+    "ci": _sb(416, I32), "cj": _sb(416, I32), "ii": _sb(128, I32),
+    "pi": _sb(1, I32), "pa": _sb(1, I32), "pb": _sb(1, I32), "pk": _sb(1, I32),
+    "pf": _sb(1, F32), "mo": _sb(1, F32), "me": _sb(1, F32), "fr": _sb(1, F32), "kf": _sb(1, F32),
+    "ha": _sb(1, F32), "s2": _sb(1, F32),
+    "nn": _sb(256, I32), "mk": _sb(256, F32), "rs": _sb(256, F32),
+    "gi": _sb(40, I32), "gj": _sb(40, I32), "gk": _sb(40, I32), "cm": _sb(40, F32), "ca": _sb(8, F32), "cb": _sb(8, F32), "r8": _sb(40, F32),
+    "li": _sb(60, I32), "lu": _sb(60, U16), "vi": _sb(40, I32), "vu": _sb(40, U16),
+    "oi": _sb(16, I32), "ou": _sb(16, U16), "ui": _sb(8, I32), "uu": _sb(8, U16),
+    "onc": _sb(128, MXW), "ons": _sb(128, U8), "bq": _sb(128, MXW), "bs": _sb(128, U8),
+    "ra": _sb(100, I32), "rb": _sb(100, I32), "rc": _sb(100, I32), "rd": _sb(100, I32),
+    "ru": _sb(100, U16), "rf": _sb(100, F32), "eg": _sb(960, F32),
+    "io2": _sb(1920, F32), "iv": _sb(320, F32), "ew": _sb(2432, F32), "w1": _sb(3072, F32),
+    "pe": _sb(1792, F32), "k2": _sb(320, F32), "xc": _sb(256, F32), "xd": _sb(256, F32),
+    "c1": _sb(16, F32), "t1": _sb(16, F32), "z1": _sb(16, F32), "z2": _sb(16, F32),
+    "cp": _sb(40, F32), "cs": _sb(40, F32), "acs": _sb(24, F32),
+    "a0": _sb(8, F32), "a1": _sb(8, F32), "l1": _sb(8, U16), "kg": _sb(128, F32), "ks": _sb(128, F32),
+    "x1": _sb(8, F32), "x2": _sb(8, F32), "x3": _sb(8, F32), "x4": _sb(8, F32), "x5": _sb(8, F32), "x6": _sb(8, F32),
+    "l2": _sb(8, U16), "fg": _sb(128, F32), "fs": _sb(128, F32), "l3": _sb(8, U16), "l4": _sb(8, U16),
+    "gt": _sb(512, BF), "yo": _sb(512, BF), "zl": _sb(512, BF), "xt": _sb(1024, BF), "ys": _sb(256, F32),
+    "yq": _sb(128, MXW), "yp": _sb(128, U8), "zq": _sb(128, MXW), "zp": _sb(128, U8),
+}
+for _b in range(4):
+    SCRATCH["dw%d" % _b] = _sb(1792, BF)
+    SCRATCH["tm%d" % _b] = _sb(128, F32)
+    SCRATCH["xq%d" % _b] = _sb(256, MXW)
+    SCRATCH["xs%d" % _b] = _sb(256, U8)
+for _n, _d in (("gq", MXW), ("gs", U8), ("rq", MXW), ("rp", U8)):
+    SCRATCH[_n] = _sb(384, _d)
+for _n, _w, _d in (("ec", 1664, MXW), ("es", 1664, U8), ("ic", 1024, MXW), ("ip", 1024, U8)):
+    SCRATCH[_n] = _sb(_w, _d)
+
+SEMAPHORES = ["cv", "cs", "ct", "cg", "dr", "dx", "du", "dv", "dw", "do", "dp"] + ["ar%d" % t for t in range(3)] + ["lo%d" % t for t in range(3)]
+
+
+def _tracker(g, T):
+    queue = {"v": g.vector, "s": g.scalar, "t": g.tensor, "g": g, "y": g.sync}
+    mine = {"v": "cv", "s": "cs", "t": "ct", "g": "cg"}
+    count, total = {"v": 0, "s": 0, "t": 0, "g": 0}, {}
+    seen = {e: {} for e in queue}
+    wrote, read = {}, {}
+
+    def need(e, tok):
+        sem, n = tok
+        n = total[sem] if n is None else n
+        if seen[e].get(sem, 0) < n:
+            queue[e].wait_ge(T.sem[sem], n)
+            seen[e][sem] = n
+
+    def order(e, rd, wr):
+        own, best = mine.get(e), {}
+        for k in rd:
+            if k in wrote and not (e == "t" and wrote[k][0] == own):
+                need_tok(best, wrote[k])
+        for k in wr:
+            if k in wrote and not (e == "t" and wrote[k][0] == own):
+                need_tok(best, wrote[k])
+            for tok in read.get(k, ()):
+                if tok[0] != own:
+                    need_tok(best, tok)
+        for sem in best:
+            need(e, (sem, best[sem]))
+
+    def need_tok(best, tok):
+        sem, n = tok
+        n = total[sem] if n is None else n
+        best[sem] = max(best.get(sem, 0), n)
+
+    def note(tok, rd, wr):
+        for k in rd:
+            read.setdefault(k, []).append(tok)
+        for k in wr:
+            wrote[k] = tok
+            read[k] = []
+
+    def op(e, fn, rd, wr):
+        order(e, rd, wr)
+        fn(queue[e]).then_inc(T.sem[mine[e]], 1)
+        count[e] += 1
+        total[mine[e]] = count[e]
+        note((mine[e], count[e]), rd, wr)
+
+    def dma(e, out, in_, sem, rd, wr):
+        order(e, rd, wr)
+        queue[e].dma_start(out, in_).then_inc(T.sem[sem], 16)
+        total[sem] = total.get(sem, 0) + 16
+        note((sem, None), rd, wr)
+
+    def send(out, in_, sem, lsem, addr, mask, n, rd):
+        order("g", rd, ())
+        g.remote_dma(out, in_, T.sem[sem], T.sem[lsem], addr[1], addr[0], mask)
+        total[lsem] = total.get(lsem, 0) + n
+        total[sem] = total.get(sem, 0) + n
+
+    def landed(sem, wr):
+        note((sem, None), (), wr)
+
+    def finish():
+        for sem in total:
+            need("y", (sem, None))
+
+    return op, dma, send, landed, finish
+
+
+def rank_program(g, core, T, topo):
+    rank = T.rank_of(core)
+    if rank is None:
+        return
+    op, dma, send, landed, finish = _tracker(g, T)
+    partner = [T.cores[rank ^ m] for m in MASKS]
+    emask = 0xFFFFFFFF
+    for d in partner:
+        emask &= topo.mask(core, d)
+    engines = bin(emask).count("1")
+    COPY, IDENT = F.Copy, F.Identity
+
+    def iota(name, a, b, pattern, base, cm, f32=False):
+        def fn(q):
+            if f32:
+                return q.iota(T[name][:, a:b], pattern, base, cm, allow_small_or_imprecise_dtypes=True)
+            return q.iota(T[name][:, a:b], pattern, base, cm)
+        op("g", fn, (), (name,))
+
+    def ts(out, in0, s1, op0, rd, wr, s2=None, op1=None):
+        if op1 is None:
+            op("v", lambda q: q.tensor_scalar(out, in0, s1, None, op0), rd, wr)
+        else:
+            op("v", lambda q: q.tensor_scalar(out, in0, s1, s2, op0, op1), rd, wr)
+
+    def tt(out, in0, in1, o, rd, wr):
+        op("v", lambda q: q.tensor_tensor(out, in0, in1, o), rd, wr)
+
+    def vcopy(out, in_, rd, wr):
+        op("v", lambda q: q.tensor_copy(out, in_), rd, wr)
+
+    def act(out, in_, rd, wr, bias=None, scale=None):
+        if bias is None and scale is None:
+            op("s", lambda q: q.activation(out, in_, COPY), rd, wr)
+        elif bias is None:
+            op("s", lambda q: q.activation(out, in_, COPY, scale=scale), rd, wr)
+        else:
+            op("s", lambda q: q.activation(out, in_, IDENT, bias=bias, scale=1.0), rd, wr)
+
+    def quant(out, sc, in_, rd, wr):
+        op("v", lambda q: q.quantize_mx(out, sc, in_), rd, wr)
+
+    def mm(bank, n, l, ls, r, rs_, rd, start=True, stop=True):
+        out = T.ps[:, 512 * bank:512 * bank + n]
+        op("t", lambda q: q.matmul_mx(out, l, ls, r, rs_, start, stop), rd, ("b%d" % bank,))
+
+    def bank(i, n):
+        return T.ps[:, 512 * i:512 * i + n]
+
+    def scan(out, d0, d1, rd, wr):
+        op("v", lambda q: q.tensor_tensor_scan(out, d0, d1, 0.0, A.mult, A.add), rd, wr)
+
+    dma("s", T.xb[:], T.x[:], "dx", (), ("xb",))
+    for d in range(-2, 4):
+        c = 20 * (d + 2)
+        lo, hi = max(0, -16 * d), min(128, 128 - 16 * d)
+        dma("y", T.rl[lo:hi, c:c + 20], T.ring[lo + 16 * d:hi + 16 * d, :], "dr", (), ("rl",))
+        if d < 0:
+            dma("y", T.rl[0:lo, c:c + 20], T.ring[128 - lo:128, :], "dr", (), ("rl%d" % d,))
+        if d > 0:
+            dma("y", T.rl[hi:128, c:c + 20], T.ring[0:128 - hi, :], "dr", (), ("rl%d" % d,))
+    dma("s", T.ub[:], T.u[:], "du", (), ("ub",))
+    dma("y", T.wq[:].bitcast(dt.uint8), T.wc[:], "dw", (), ("wq",))
+    dma("y", T.wp[:], T.ws[:], "dw", (), ("wp",))
+    dma("y", T.vb[:], T.v[:], "dv", (), ("vb",))
+
+    op("v", lambda q: q.memset(T.et[:], 0.0), (), ("et",))
+    iota("pi", 0, 1, [[0, 1]], 0, 1)
+    iota("ci", 0, 224, [[32, 7], [0, 2], [1, 16]], 96, 0)
+    op("g", lambda q: q.iota(T.ci[:, 224:416], [[32, 6], [0, 2], [1, 16]], 112, 0), (), ("ci_",))
+    iota("ui", 0, 8, [[0, 8]], 0, 16)
+    iota("io2", 0, 960, [[1, 960]], 0, 0, True)
+    iota("nn", 0, 256, [[0, 16], [1, 16]], 0, 0)
+    iota("li", 0, 60, [[40, 3], [2, 10], [0, 2]], 0, 0)
+    op("g", lambda q: q.iota(T.w1[:, 1280:3072], [[128, 7], [1, 256]], 1664, 0, allow_small_or_imprecise_dtypes=True), (), ("po",))
+    iota("gi", 0, 40, [[0, 5], [1, 8]], 8, 0)
+    iota("iv", 0, 320, [[-1, 320]], 959, 0, True)
+    iota("oi", 0, 16, [[16, 16]], 0, 0)
+    iota("vi", 0, 40, [[0, 2], [-16, 20]], 319, 0)
+    iota("ii", 0, 128, [[1, 128]], 0, 0)
+
+    ts(T.pa[:], T.pi[:], 4, A.arith_shift_right, ("pi",), ("pa",), 1, A.bitwise_and)
+    ts(T.pb[:], T.pi[:], 5, A.arith_shift_right, ("pi",), ("pb",))
+    ts(T.pk[:], T.pi[:], 15, A.bitwise_and, ("pi",), ("pk",))
+    vcopy(T.pf[:], T.pi[:], ("pi",), ("pf",))
+    vcopy(T.mo[:], T.pa[:], ("pa",), ("mo",))
+    ts(T.me[:], T.pa[:], -1.0, A.mult, ("pa",), ("me",), 1.0, A.add)
+    ts(T.fr[:], T.pb[:], -512.0, A.mult, ("pb",), ("fr",), 2560.0, A.add)
+    vcopy(T.kf[:], T.pk[:], ("pk",), ("kf",))
+    ts(T.ha[:], T.pb[:], -2.0, A.mult, ("pb",), ("ha",))
+    ts(T.s2[:], T.mo[:], 256.0, A.mult, ("mo", "kf"), ("s2",), T.kf[:, 0:1], A.add)
+    ts(T.cj[:], T.ci[:], 127, A.bitwise_and, ("ci", "ci_"), ("cj",))
+    ts(T.et[:, 3:1667:4], T.cj[:], T.pf[:, 0:1], A.is_equal, ("cj", "pf"), ("et",))
+    for b in range(4):
+        quant(T.ec[:, 416 * b:416 * b + 416], T.es[:, 416 * b:416 * b + 416], T.et[:, 3 - b:1667 - b], ("et",), ("ec%d" % b,))
+    rl = ["rl"] + ["rl%d" % d for d in (-2, -1, 1, 2, 3)]
+    ts(T.ra[:], T.rl[:, 20:120], T.me[:, 0:1], A.mult, rl + ["me", "fr"], ("ra",), T.fr[:, 0:1], A.add)
+    ts(T.rb[:], T.rl[:, 0:100], T.mo[:, 0:1], A.mult, rl + ["mo"], ("rb",))
+    tt(T.rc[:], T.ra[:], T.rb[:], A.add, ("ra", "rb"), ("rc",))
+    ts(T.rd[:], T.rc[:], 2047, A.bitwise_and, ("rc",), ("rd",))
+    vcopy(T.ru[:], T.rd[:], ("rd",), ("ru",))
+    vcopy(T.rf[:], T.rd[:], ("rd",), ("rf",))
+    ts(T.lu[:], T.li[:], T.mo[:, 0:1], A.add, ("li", "mo"), ("lu",))
+    xq, xs = T.xq0, T.xs0
+    quant(xq[:], xs[:], T.xb[:], ("xb",), ("xq0l", "xq0e"))
+    quant(T.uq[:], T.us[:], T.ub[:], ("ub",), ("uq",))
+    op("v", lambda q: q.tensor_scalar(T.ui[:], T.ui[:], 112, None, A.bitwise_and), ("ui",), ("ui",))
+    vcopy(T.uu[:], T.ui[:], ("ui",), ("uu",))
+    op("v", lambda q: q.tensor_copy(T.uq2[:].bitcast(dt.uint32), T.uq[:].bitcast(dt.uint32).indirect(T.uu[:])), ("uq", "uu"), ("uq2",))
+    op("v", lambda q: q.tensor_copy(T.us2[:], T.us[:].indirect(T.uu[:])), ("uq", "uu"), ("us2",))
+    op("v", lambda q: q.memset(T.bt[:], 0.0), (), ("bt0", "bt1"))
+    op("v", lambda q: q.memset(T.ot[:], 1.0), (), ("ot",))
+    quant(T.onc[:], T.ons[:], T.ot[:], ("ot",), ("on",))
+
+    act(T.io2[:, 960:1920], T.io2[:, 0:960], ("io2",), ("io3",), bias=960.0)
+    act(T.pe[:, 512:1024], T.io2[:, 512:1024], ("io2", "io3"), ("pe",), bias=1280.0)
+    act(T.ew[:, 1920:2176], T.io2[:, 512:768], ("io2", "io3"), ("ew_a",))
+    act(T.ew[:, 2176:2432], T.io2[:, 1024:1280], ("io2", "io3"), ("ew_b",))
+    act(T.eg[:], T.rf[:].indirect(T.lu[:]), ("rf", "lu"), ("eg",))
+
+    SP, VP, MP = [0, 1, 2, 3], [4, 5], [6, 7]
+    turn = {"s": 0, "v": 0, "m": 0}
+
+    def nextbank(k):
+        pool = {"s": SP, "v": VP, "m": MP}[k]
+        turn[k] += 1
+        return pool[(turn[k] - 1) % len(pool)]
+
+    ALL = [(s, b) for s in range(7) for b in range(4)]
+    DWK = [["dw%d_%d%s" % (b, s, h) for s in range(7) for h in "le"] for b in range(4)]
+
+    def slot(e, k, sig, b, halves):
+        lo, hi = (0 if "l" in halves else 128), (256 if "e" in halves else 128)
+        n = hi - lo
+        off = 16 * sig if sig % 2 == 0 else 224 + 16 * (sig - 1)
+        bk = nextbank(e)
+        names = ["dw%d_%d%s" % (b, sig, h) for h in halves]
+        q, s = T["xq%d" % k], T["xs%d" % k]
+        off += 416 * b
+        mm(bk, n, T.ec[:, off:off + 128], T.es[:, off:off + 128], q[:, lo:hi], s[:, lo:hi],
+           ["ec%d" % b] + ["xq%d%s" % (k, h) for h in halves])
+
+        def copy():
+            out = T["dw%d" % b][:, 256 * sig + lo:256 * sig + hi]
+            if e == "v":
+                vcopy(out, bank(bk, n), ("b%d" % bk,), names)
+            else:
+                act(out, bank(bk, n), ("b%d" % bk,), names)
+        return copy
+
+    def scores(k, h):
+        lo = 0 if h == "l" else 128
+        bk = nextbank("m")
+        mm(bk, 128, T["xq%d" % k][:, lo:lo + 128], T["xs%d" % k][:, lo:lo + 128], T.uq2[:], T.us2[:], ("xq%d%s" % (k, h), "uq2", "us2"))
+        i = 0 if h == "l" else 1
+        return lambda: ts(T.bt[:, i:160:4], bank(bk, 40), 0.0, A.is_gt, ("b%d" % bk,), ("bt%d" % i,))
+
+    def lists(hf, dst):
+        m = slice(8 * hf, 8 * hf + 8)
+        ts(T.a0[:], T.t1[:, m], T.cs[:, 7:8], A.min, ("t1", "cs"), ("a0",), T.cs[:, 15:16], A.max)
+        tt(T.a1[:], T.c1[:, m], T.a0[:], A.subtract, ("c1", "a0"), ("a1",))
+        vcopy(T.l1[:], T.a1[:], ("a1",), ("l1",))
+        tt(T.kg[:], T.w1[:, 0:3072].indirect(T.l1[:]), T.mk[:, 0:128], A.mult, ("w1", "po", "l1", "mk"), ("kg",))
+        scan(T.ks[:], T.rs[:, 0:128], T.kg[:], ("rs", "kg"), ("ks",))
+        v = T.ks[:, 15:128:16]
+        ts(T.x1[:], v, 1920.0, A.is_lt, ("ks", "cs"), ("x1",), T.cs[:, 23:24], A.mult)
+        ts(T.x2[:], v, 1280.0, A.is_lt, ("ks", "cs"), ("x2",), T.cs[:, 31:32], A.mult)
+        ts(T.x3[:], v, 640.0, A.is_lt, ("ks", "cs"), ("x3",), T.cs[:, 39:40], A.mult)
+        tt(T.x4[:], v, T.x1[:], A.subtract, ("ks", "x1"), ("x4",))
+        tt(T.x5[:], T.x2[:], T.x3[:], A.add, ("x2", "x3"), ("x5",))
+        tt(T.x6[:], T.x4[:], T.x5[:], A.subtract, ("x4", "x5"), ("x6",))
+        vcopy(T.l2[:], T.x6[:], ("x6",), ("l2",))
+        tt(T.fg[:], T.ew[:, 0:2432].indirect(T.l2[:]), T.mk[:, 0:128], A.mult, ("ew", "ew_a", "ew_b", "ew0", "ew1", "ew2", "l2", "mk"), ("fg",))
+        scan(T.fs[:], T.rs[:, 0:128], T.fg[:], ("rs", "fg"), ("fs",))
+        vcopy(T[dst][:], T.fs[:, 15:128:16], ("fs",), (dst,))
+
+    def gather(buf, dst):
+        for b in range(4):
+            out, src = T[buf][:, b:512:4], T["dw%d" % b][:, 0:1792].indirect(T[dst][:])
+            if b % 2:
+                act(out, src, DWK[b] + [dst], ("%s_%d" % (buf, b),))
+            else:
+                vcopy(out, src, DWK[b] + [dst], ("%s_%d" % (buf, b),))
+
+    def tables():
+        for r, c in enumerate((0, 40, 80)):
+            op("v", lambda q, r=r, c=c: q.tensor_copy(T.w1[:, 1280:3072].indirect(T.ru[:, c:c + 20]), T.io2[:, 640 * r + 320:640 * r + 640]),
+               ("ru", "io2", "io3"), ("po",))
+        act(T.w1[:, 320:640], T.w1[:, 1280:3072].indirect(T.ru[:, 20:40]), ("po", "ru"), ("w1",))
+        act(T.k2[:], T.w1[:, 1280:3072].indirect(T.ru[:, 60:80]), ("po", "ru"), ("k2",))
+        op("v", lambda q: q.tensor_copy(T.pe[:].indirect(T.ru[:, 20:40]), T.io2[:, 320:640]), ("ru", "io2"), ("pe",))
+        op("v", lambda q: q.tensor_copy(T.pe[:].indirect(T.ru[:, 60:80]), T.iv[:]), ("ru", "iv"), ("pe",))
+        ts(T.vu[:], T.vi[:], T.kf[:, 0:1], A.subtract, ("vi", "kf"), ("vu",))
+        act(T.w1[:, 0:320], T.w1[:, 320:640], ("w1",), ("w1",))
+        act(T.w1[:, 640:1280], T.k2[:].indirect(T.vu[:]), ("k2", "vu"), ("w1",))
+        for r in range(3):
+            op("v", lambda q, r=r: q.transpose(T.ew[:, 640 * r + 320:640 * r + 640], T.eg[:, 320 * r:320 * r + 320]), ("eg",), ("ew%d" % r,))
+            act(T.ew[:, 640 * r:640 * r + 320], T.ew[:, 640 * r + 320:640 * r + 640], ("ew%d" % r,), ("ew",))
+        ts(T.ou[:], T.oi[:], T.s2[:, 0:1], A.add, ("oi", "s2"), ("ou",))
+        ts(T.mk[:], T.nn[:], T.kf[:, 0:1], A.is_equal, ("nn", "kf"), ("mk",))
+        ts(T.rs[:], T.nn[:], 0.0, A.not_equal, ("nn",), ("rs",))
+        tt(T.xc[:], T.pe[:, 512:1024].indirect(T.ou[:]), T.mk[:], A.mult, ("pe", "ou", "mk"), ("xc",))
+        scan(T.xd[:], T.rs[:], T.xc[:], ("rs", "xc"), ("xd",))
+        vcopy(T.c1[:], T.xd[:, 15:256:16], ("xd",), ("c1",))
+        ts(T.z1[:], T.c1[:], 1280.0, A.is_lt, ("c1",), ("z1",), -4096.0, A.mult)
+        ts(T.z2[:], T.c1[:], 640.0, A.is_lt, ("c1",), ("z2",), 8192.0, A.mult)
+        tt(T.t1[:], T.z1[:], T.z2[:], A.add, ("z1", "z2"), ("t1",))
+
+    def countmask():
+        ts(T.gj[:], T.gi[:], T.ha[:, 0:1], A.add, ("gi", "ha"), ("gj",))
+        ts(T.gk[:], T.gj[:], 7, A.bitwise_and, ("gj",), ("gk",))
+        ts(T.r8[:], T.gi[:], 8.0, A.not_equal, ("gi",), ("r8",))
+        ts(T.cm[:, 0:8], T.gk[:, 0:8], 0.0, A.is_equal, ("gk",), ("cm0",))
+        ts(T.cm[:, 8:16], T.gk[:, 8:16], 2.0, A.is_equal, ("gk",), ("cm1",), -1.0, A.mult)
+        ts(T.cm[:, 16:24], T.gk[:, 16:24], 3.0, A.is_equal, ("gk",), ("cm2",))
+        ts(T.ca[:], T.gk[:, 24:32], 1.0, A.is_equal, ("gk",), ("ca",))
+        ts(T.cb[:], T.gk[:, 32:40], 7.0, A.is_equal, ("gk",), ("cb",))
+        tt(T.cm[:, 24:32], T.ca[:], T.cm[:, 16:24], A.subtract, ("ca", "cm2"), ("cm3",))
+        tt(T.cm[:, 32:40], T.cb[:], T.ca[:], A.subtract, ("cb", "ca"), ("cm4",))
+
+    for t in range(3):
+        k = t
+        is_late = scores(k, "l")
+        is_early = scores(k, "e") if t == 0 else None
+        halves = "le" if t == 0 else "l"
+        nv = NV_R0 if t == 0 else NV_LATE
+        first = [slot("v", k, s, b, halves) for s, b in ALL[:NV_FIRST]]
+        mids = [slot("s", k, s, b, halves) for s, b in ALL[NV_FIRST:NV_FIRST + 4]]
+        is_late()
+        if is_early:
+            is_early()
+        quant(T.bq[:], T.bs[:], T.bt[:], ("bt0", "bt1"), ("bq",))
+        bc = nextbank("m")
+        mm(bc, 128, T.onc[:], T.ons[:], T.bq[:], T.bs[:], ("on", "bq"))
+        for c in first:
+            c()
+        if t == 0:
+            countmask()
+        tt(T.cp[:], bank(bc, 40), T.cm[:], A.mult, ("b%d" % bc, "cm0", "cm1", "cm2", "cm3", "cm4"), ("cp",))
+        scan(T.cs[:], T.r8[:], T.cp[:], ("r8", "cp"), ("cs",))
+        vcopy(T.acs[:, t:24:3], bank(bc, 8), ("b%d" % bc,), ("acs",))
+        for c in mids:
+            c()
+        rest = ALL[NV_FIRST + 4:]
+        nrest = len(rest) - (nv - NV_FIRST)
+        for i, (s, b) in enumerate(rest[:nrest]):
+            if t == 0 and i == NS_TABLES:
+                tables()
+            slot("s", k, s, b, halves)()
+        lists(0, "l3")
+        for s, b in rest[nrest:]:
+            slot("v", k, s, b, halves)()
+        gather("gt", "l3")
+        w = slice(128 * t, 128 * t + 128)
+        quant(T.gq[:, w], T.gs[:, w], T.gt[:], ["gt_%d" % b for b in range(4)], ("gq%d" % t,))
+        addr = topo.addr(partner[t])
+        send(T.rq[:, w].bitcast(dt.uint8), T.gq[:, w].bitcast(dt.uint8), "ar%d" % t, "lo%d" % t, addr, emask, engines, ("gq%d" % t,))
+        send(T.rp[:, w], T.gs[:, w], "ar%d" % t, "lo%d" % t, addr, emask, engines, ("gq%d" % t,))
+        landed("ar%d" % t, ("rq%d" % t,))
+        lists(1, "l4")
+        gather("yo", "l4")
+        YO = ["yo_%d" % b for b in range(4)]
+        quant(T.yq[:], T.yp[:], T.yo[:], YO, ("yq",))
+        n = k + 1
+        for b in range(4):
+            bk = nextbank("s")
+            mm(bk, 128, T.wq[:, 128 * b:128 * b + 128], T.wp[:, 128 * b:128 * b + 128], T.yq[:], T.yp[:], ("wq", "wp", "yq"))
+            act(T["tm%d" % b][:], bank(bk, 128), ("b%d" % bk,), ("tm%d" % b,), scale=0.03125)
+            tt(T.xt[:, 512 + b:1024:4], T["tm%d" % b][:], T.yo[:, b:512:4], A.add, ("tm%d" % b, YO[b]), ("xe%d" % b,))
+        quant(T["xq%d" % n][:, 128:256], T["xs%d" % n][:, 128:256], T.xt[:, 512:1024], ["xe%d" % b for b in range(4)], ("xq%de" % n,))
+        if t == 0:
+            op("v", lambda q: q.memset(T.it[:], 0.0), (), ("it",))
+            ts(T.it[:, 3:515:4], T.ii[:], T.pf[:, 0:1], A.is_equal, ("ii", "pf"), ("it",))
+            ts(T.it[:, 515:1027:4], T.ii[:], T.pf[:, 0:1], A.is_equal, ("ii", "pf"), ("it",), 32.0, A.mult)
+            for b in range(4):
+                quant(T.ic[:, 256 * b:256 * b + 256], T.ip[:, 256 * b:256 * b + 256], T.it[:, 3 - b:1027 - b], ("it",), ("ic%d" % b,))
+            quant(T.vq[:], T.vs[:], T.vb[:], ("vb",), ("vq",))
+        if n < 3:
+            scores(n, "e")()
+            for i, (s, b) in enumerate(ALL):
+                slot("v" if i * NV_EARLY // 28 != (i + 1) * NV_EARLY // 28 else "s", n, s, b, "e")()
+        else:
+            mm(6, 128, T.vq[:], T.vs[:], T.xq3[:, 128:256], T.xs3[:, 128:256], ("vq", "xq3e"))
+            vcopy(T.ys[:, 128:256], bank(6, 128), ("b6",), ("yse",))
+            dma("y", T.y[:, 128:256], T.ys[:, 128:256], "do", ("yse",), ())
+            dma("y", T.oc[:, 512:1024], T.xq3[:, 128:256].bitcast(dt.uint8), "do", ("xq3e",), ())
+            for i in range(4):
+                dma("y", T.osc[4 * i:4 * i + 4, 128:256], T.xs3[32 * i:32 * i + 4, 128:256], "do", ("xq3e",), ())
+            dma("y", T.ac[:], T.acs[0:1, 0:24], "do", ("acs",), ())
+        rq, rp = T.rq[:, w], T.rp[:, w]
+        ub = [0, 4, 1, 5]
+        rb = [2, 6, 3, 7]
+        for b in range(4):
+            mm(ub[b], 128, T.ic[:, 256 * b:256 * b + 128], T.ip[:, 256 * b:256 * b + 128], rq, rp, ("ic%d" % b, "rq%d" % t))
+        for b in range(4):
+            mm(rb[b], 128, T.ic[:, 256 * b + 128:256 * b + 256], T.ip[:, 256 * b + 128:256 * b + 256], rq, rp, ("ic%d" % b, "rq%d" % t), True, False)
+        for b in range(4):
+            if b % 2:
+                vcopy(T.zl[:, b:512:4], bank(ub[b], 128), ("b%d" % ub[b],), ("zl%d" % b,))
+            else:
+                act(T.zl[:, b:512:4], bank(ub[b], 128), ("b%d" % ub[b],), ("zl%d" % b,))
+        quant(T.zq[:], T.zp[:], T.zl[:], ["zl%d" % b for b in range(4)], ("zq",))
+        for b in range(4):
+            mm(rb[b], 128, T.wq[:, 128 * b:128 * b + 128], T.wp[:, 128 * b:128 * b + 128], T.zq[:], T.zp[:], ("wq", "wp", "zq"), False, True)
+        for b in range(4):
+            if b % 2:
+                ts(T.xt[:, b:512:4], bank(rb[b], 128), 0.03125, A.mult, ("b%d" % rb[b],), ("xl%d" % b,))
+            else:
+                act(T.xt[:, b:512:4], bank(rb[b], 128), ("b%d" % rb[b],), ("xl%d" % b,), scale=0.03125)
+        quant(T["xq%d" % n][:, 0:128], T["xs%d" % n][:, 0:128], T.xt[:, 0:512], ["xl%d" % b for b in range(4)], ("xq%dl" % n,))
+    mm(7, 128, T.vq[:], T.vs[:], T.xq3[:, 0:128], T.xs3[:, 0:128], ("vq", "xq3l"))
+    vcopy(T.ys[:, 0:128], bank(7, 128), ("b7",), ("ysl",))
+    dma("s", T.oc[:, 0:512], T.xq3[:, 0:128].bitcast(dt.uint8), "dp", ("xq3l",), ())
+    for i in range(4):
+        dma("y" if i < 2 else "s", T.osc[4 * i:4 * i + 4, 0:128], T.xs3[32 * i:32 * i + 4, 0:128], "dp", ("xq3l",), ())
+    dma("y", T.y[:, 0:128], T.ys[:, 0:128], "dp", ("ysl",), ())
+    finish()

@@ -1,9 +1,8 @@
 from concourse.mybir import dt, AluOpType as A, ActivationFunctionType as F
 
 MASKS = [1, 2, 4]
-NV_FIRST, NV_LATE, NV_EARLY = 2, 6, 14
-NV_R0 = 6
-NS_TABLES = 10
+NV_LATE, NV_EARLY = 12, 14
+NV_R0, NS_TABLES = 6, 12
 
 F32, BF, I32, U16, U8, MXW = "float32", "bfloat16", "int32", "uint16", "uint8", "float8_e4m3fn_x4"
 
@@ -25,7 +24,7 @@ SCRATCH = {
     "nn": _sb(256, I32), "mk": _sb(256, F32), "rs": _sb(256, F32),
     "gi": _sb(40, I32), "gj": _sb(40, I32), "gk": _sb(40, I32), "cm": _sb(40, F32), "ca": _sb(8, F32), "cb": _sb(8, F32), "r8": _sb(40, F32),
     "li": _sb(60, I32), "lu": _sb(60, U16), "vi": _sb(40, I32), "vu": _sb(40, U16),
-    "oi": _sb(16, I32), "ou": _sb(16, U16), "ui": _sb(8, I32), "uu": _sb(8, U16),
+    "oi": _sb(16, I32), "ou": _sb(16, U16), "ui": _sb(8, I32), "uj": _sb(8, I32), "uu": _sb(8, U16),
     "onc": _sb(128, MXW), "ons": _sb(128, U8), "bq": _sb(128, MXW), "bs": _sb(128, U8),
     "ra": _sb(100, I32), "rb": _sb(100, I32), "rc": _sb(100, I32), "rd": _sb(100, I32),
     "ru": _sb(100, U16), "rf": _sb(100, F32), "eg": _sb(960, F32),
@@ -33,10 +32,10 @@ SCRATCH = {
     "pe": _sb(1792, F32), "k2": _sb(320, F32), "xc": _sb(256, F32), "xd": _sb(256, F32),
     "c1": _sb(16, F32), "t1": _sb(16, F32), "z1": _sb(16, F32), "z2": _sb(16, F32),
     "cp": _sb(40, F32), "cs": _sb(40, F32), "acs": _sb(24, F32),
-    "a0": _sb(8, F32), "a1": _sb(8, F32), "l1": _sb(8, U16), "kg": _sb(128, F32), "ks": _sb(128, F32),
-    "x1": _sb(8, F32), "x2": _sb(8, F32), "x3": _sb(8, F32), "x4": _sb(8, F32), "x5": _sb(8, F32), "x6": _sb(8, F32),
-    "l2": _sb(8, U16), "fg": _sb(128, F32), "fs": _sb(128, F32), "l3": _sb(8, U16), "l4": _sb(8, U16),
-    "gt": _sb(512, BF), "yo": _sb(512, BF), "zl": _sb(512, BF), "xt": _sb(1024, BF), "ys": _sb(256, F32),
+    "a0": _sb(16, F32), "a1": _sb(16, F32), "l1": _sb(16, U16), "kg": _sb(256, F32), "ks": _sb(256, F32),
+    "x1": _sb(16, F32), "x2": _sb(16, F32), "x3": _sb(16, F32), "x4": _sb(16, F32), "x5": _sb(16, F32), "x6": _sb(16, F32),
+    "l2": _sb(16, U16), "fg": _sb(256, F32), "fs": _sb(256, F32), "l3": _sb(16, U16),
+    "gt": _sb(512, BF), "yo": _sb(512, BF), "y32": _sb(512, BF), "zl": _sb(512, BF), "xt": _sb(1024, BF), "ys": _sb(256, F32),
     "yq": _sb(128, MXW), "yp": _sb(128, U8), "zq": _sb(128, MXW), "zp": _sb(128, U8),
 }
 for _b in range(4):
@@ -66,24 +65,24 @@ def _tracker(g, T):
             queue[e].wait_ge(T.sem[sem], n)
             seen[e][sem] = n
 
+    def merge(best, tok):
+        sem, n = tok
+        n = total[sem] if n is None else n
+        best[sem] = max(best.get(sem, 0), n)
+
     def order(e, rd, wr):
         own, best = mine.get(e), {}
         for k in rd:
             if k in wrote and not (e == "t" and wrote[k][0] == own):
-                need_tok(best, wrote[k])
+                merge(best, wrote[k])
         for k in wr:
             if k in wrote and not (e == "t" and wrote[k][0] == own):
-                need_tok(best, wrote[k])
+                merge(best, wrote[k])
             for tok in read.get(k, ()):
                 if tok[0] != own:
-                    need_tok(best, tok)
+                    merge(best, tok)
         for sem in best:
             need(e, (sem, best[sem]))
-
-    def need_tok(best, tok):
-        sem, n = tok
-        n = total[sem] if n is None else n
-        best[sem] = max(best.get(sem, 0), n)
 
     def note(tok, rd, wr):
         for k in rd:
@@ -127,18 +126,21 @@ def rank_program(g, core, T, topo):
         return
     op, dma, send, landed, finish = _tracker(g, T)
     partner = [T.cores[rank ^ m] for m in MASKS]
-    emask = 0xFFFFFFFF
+    emask = topo.mask(core, partner[0])
     for d in partner:
         emask &= topo.mask(core, d)
     engines = bin(emask).count("1")
     COPY, IDENT = F.Copy, F.Identity
 
-    def iota(name, a, b, pattern, base, cm, f32=False):
+    def iota(name, a, b, pattern, base, cm, f32=False, key=None):
         def fn(q):
             if f32:
                 return q.iota(T[name][:, a:b], pattern, base, cm, allow_small_or_imprecise_dtypes=True)
             return q.iota(T[name][:, a:b], pattern, base, cm)
-        op("g", fn, (), (name,))
+        op("g", fn, (), (key or name,))
+
+    def gcopy(out, in_, n, rd, wr):
+        op("g", lambda q: q.affine_select(out, in_, [[0, n]], A.is_gt, 0.0, 1, 0), rd, wr)
 
     def ts(out, in0, s1, op0, rd, wr, s2=None, op1=None):
         if op1 is None:
@@ -173,81 +175,81 @@ def rank_program(g, core, T, topo):
     def scan(out, d0, d1, rd, wr):
         op("v", lambda q: q.tensor_tensor_scan(out, d0, d1, 0.0, A.mult, A.add), rd, wr)
 
+    def memset(name, val, keys):
+        op("v", lambda q: q.memset(T[name][:], val), (), keys)
+
     dma("s", T.xb[:], T.x[:], "dx", (), ("xb",))
+    RL = []
     for d in range(-2, 4):
         c = 20 * (d + 2)
         lo, hi = max(0, -16 * d), min(128, 128 - 16 * d)
-        dma("y", T.rl[lo:hi, c:c + 20], T.ring[lo + 16 * d:hi + 16 * d, :], "dr", (), ("rl",))
-        if d < 0:
-            dma("y", T.rl[0:lo, c:c + 20], T.ring[128 - lo:128, :], "dr", (), ("rl%d" % d,))
-        if d > 0:
-            dma("y", T.rl[hi:128, c:c + 20], T.ring[0:128 - hi, :], "dr", (), ("rl%d" % d,))
+        for a, b, f in ((lo, hi, 16 * d), (0, lo, 128 - lo), (hi, 128, -hi)):
+            if a < b:
+                RL.append("rl%d" % len(RL))
+                dma("y", T.rl[a:b, c:c + 20], T.ring[a + f:b + f, :], "dr", (), (RL[-1],))
     dma("s", T.ub[:], T.u[:], "du", (), ("ub",))
     dma("y", T.wq[:].bitcast(dt.uint8), T.wc[:], "dw", (), ("wq",))
     dma("y", T.wp[:], T.ws[:], "dw", (), ("wp",))
     dma("y", T.vb[:], T.v[:], "dv", (), ("vb",))
 
-    op("v", lambda q: q.memset(T.et[:], 0.0), (), ("et",))
     iota("pi", 0, 1, [[0, 1]], 0, 1)
     iota("ci", 0, 224, [[32, 7], [0, 2], [1, 16]], 96, 0)
-    op("g", lambda q: q.iota(T.ci[:, 224:416], [[32, 6], [0, 2], [1, 16]], 112, 0), (), ("ci_",))
-    iota("ui", 0, 8, [[0, 8]], 0, 16)
-    iota("io2", 0, 960, [[1, 960]], 0, 0, True)
-    iota("nn", 0, 256, [[0, 16], [1, 16]], 0, 0)
+    iota("ci", 224, 416, [[32, 6], [0, 2], [1, 16]], 112, 0, key="ci_")
+    iota("io2", 0, 480, [[1, 480]], 0, 0, True)
     iota("li", 0, 60, [[40, 3], [2, 10], [0, 2]], 0, 0)
-    op("g", lambda q: q.iota(T.w1[:, 1280:3072], [[128, 7], [1, 256]], 1664, 0, allow_small_or_imprecise_dtypes=True), (), ("po",))
-    iota("gi", 0, 40, [[0, 5], [1, 8]], 8, 0)
+    iota("ui", 0, 8, [[0, 8]], 0, 16)
     iota("iv", 0, 320, [[-1, 320]], 959, 0, True)
+    iota("nn", 0, 256, [[0, 16], [1, 16]], 0, 0)
+    iota("gi", 0, 40, [[0, 5], [1, 8]], 8, 0)
     iota("oi", 0, 16, [[16, 16]], 0, 0)
     iota("vi", 0, 40, [[0, 2], [-16, 20]], 319, 0)
     iota("ii", 0, 128, [[1, 128]], 0, 0)
 
+    memset("et", 0.0, ("et",))
     ts(T.pa[:], T.pi[:], 4, A.arith_shift_right, ("pi",), ("pa",), 1, A.bitwise_and)
     ts(T.pb[:], T.pi[:], 5, A.arith_shift_right, ("pi",), ("pb",))
     ts(T.pk[:], T.pi[:], 15, A.bitwise_and, ("pi",), ("pk",))
     vcopy(T.pf[:], T.pi[:], ("pi",), ("pf",))
+    ts(T.cj[:], T.ci[:], 127, A.bitwise_and, ("ci", "ci_"), ("cj",))
     vcopy(T.mo[:], T.pa[:], ("pa",), ("mo",))
     ts(T.me[:], T.pa[:], -1.0, A.mult, ("pa",), ("me",), 1.0, A.add)
     ts(T.fr[:], T.pb[:], -512.0, A.mult, ("pb",), ("fr",), 2560.0, A.add)
+    ts(T.et[:, 3:1667:4], T.cj[:], T.pf[:, 0:1], A.is_equal, ("cj", "pf"), ("et",))
     vcopy(T.kf[:], T.pk[:], ("pk",), ("kf",))
     ts(T.ha[:], T.pb[:], -2.0, A.mult, ("pb",), ("ha",))
-    ts(T.s2[:], T.mo[:], 256.0, A.mult, ("mo", "kf"), ("s2",), T.kf[:, 0:1], A.add)
-    ts(T.cj[:], T.ci[:], 127, A.bitwise_and, ("ci", "ci_"), ("cj",))
-    ts(T.et[:, 3:1667:4], T.cj[:], T.pf[:, 0:1], A.is_equal, ("cj", "pf"), ("et",))
+    ts(T.lu[:], T.li[:], T.mo[:, 0:1], A.add, ("li", "mo"), ("lu",))
     for b in range(4):
         quant(T.ec[:, 416 * b:416 * b + 416], T.es[:, 416 * b:416 * b + 416], T.et[:, 3 - b:1667 - b], ("et",), ("ec%d" % b,))
-    rl = ["rl"] + ["rl%d" % d for d in (-2, -1, 1, 2, 3)]
-    ts(T.ra[:], T.rl[:, 20:120], T.me[:, 0:1], A.mult, rl + ["me", "fr"], ("ra",), T.fr[:, 0:1], A.add)
-    ts(T.rb[:], T.rl[:, 0:100], T.mo[:, 0:1], A.mult, rl + ["mo"], ("rb",))
+    ts(T.ra[:], T.rl[:, 20:120], T.me[:, 0:1], A.mult, RL + ["me", "fr"], ("ra",), T.fr[:, 0:1], A.add)
+    ts(T.rb[:], T.rl[:, 0:100], T.mo[:, 0:1], A.mult, RL + ["mo"], ("rb",))
+    ts(T.s2[:], T.mo[:], 256.0, A.mult, ("mo", "kf"), ("s2",), T.kf[:, 0:1], A.add)
     tt(T.rc[:], T.ra[:], T.rb[:], A.add, ("ra", "rb"), ("rc",))
+    ts(T.uj[:], T.ui[:], 112, A.bitwise_and, ("ui",), ("uj",))
     ts(T.rd[:], T.rc[:], 2047, A.bitwise_and, ("rc",), ("rd",))
+    vcopy(T.uu[:], T.uj[:], ("uj",), ("uu",))
     vcopy(T.ru[:], T.rd[:], ("rd",), ("ru",))
     vcopy(T.rf[:], T.rd[:], ("rd",), ("rf",))
-    ts(T.lu[:], T.li[:], T.mo[:, 0:1], A.add, ("li", "mo"), ("lu",))
-    xq, xs = T.xq0, T.xs0
-    quant(xq[:], xs[:], T.xb[:], ("xb",), ("xq0l", "xq0e"))
-    quant(T.uq[:], T.us[:], T.ub[:], ("ub",), ("uq",))
-    op("v", lambda q: q.tensor_scalar(T.ui[:], T.ui[:], 112, None, A.bitwise_and), ("ui",), ("ui",))
-    vcopy(T.uu[:], T.ui[:], ("ui",), ("uu",))
-    op("v", lambda q: q.tensor_copy(T.uq2[:].bitcast(dt.uint32), T.uq[:].bitcast(dt.uint32).indirect(T.uu[:])), ("uq", "uu"), ("uq2",))
-    op("v", lambda q: q.tensor_copy(T.us2[:], T.us[:].indirect(T.uu[:])), ("uq", "uu"), ("us2",))
-    op("v", lambda q: q.memset(T.bt[:], 0.0), (), ("bt0", "bt1"))
-    op("v", lambda q: q.memset(T.ot[:], 1.0), (), ("ot",))
-    quant(T.onc[:], T.ons[:], T.ot[:], ("ot",), ("on",))
+    quant(T.xq0[:], T.xs0[:], T.xb[:], ("xb",), ("xq0l", "xq0e"))
 
-    act(T.io2[:, 960:1920], T.io2[:, 0:960], ("io2",), ("io3",), bias=960.0)
-    act(T.pe[:, 512:1024], T.io2[:, 512:1024], ("io2", "io3"), ("pe",), bias=1280.0)
-    act(T.ew[:, 1920:2176], T.io2[:, 512:768], ("io2", "io3"), ("ew_a",))
-    act(T.ew[:, 2176:2432], T.io2[:, 1024:1280], ("io2", "io3"), ("ew_b",))
+    act(T.io2[:, 480:960], T.io2[:, 0:480], ("io2",), ("io3",), bias=480.0)
+    act(T.w1[:, 1280:1792], T.io2[:, 0:512], ("io2", "io3"), ("po_a",))
+    act(T.w1[:, 1792:2048], T.io2[:, 0:256], ("io2",), ("po_b",), bias=1920.0)
+    act(T.w1[:, 2048:2304], T.io2[:, 0:256], ("io2",), ("po_c",))
+    act(T.w1[:, 2304:2560], T.io2[:, 0:256], ("io2",), ("po_d",), bias=2176.0)
+    act(T.w1[:, 2560:3072], T.io2[:, 0:512], ("io2", "io3"), ("po_e",))
+    act(T.io2[:, 960:1920], T.io2[:, 0:960], ("io2", "io3"), ("io4",), bias=960.0)
+    act(T.pe[:, 512:1024], T.io2[:, 512:1024], ("io3", "io4"), ("pe",), bias=1280.0)
+    act(T.ew[:, 1920:2176], T.io2[:, 512:768], ("io3",), ("ew_a",))
+    act(T.ew[:, 2176:2432], T.io2[:, 1024:1280], ("io4",), ("ew_b",))
     act(T.eg[:], T.rf[:].indirect(T.lu[:]), ("rf", "lu"), ("eg",))
+    PO = ["po", "po_a", "po_b", "po_c", "po_d", "po_e"]
 
-    SP, VP, MP = [0, 1, 2, 3], [4, 5], [6, 7]
+    POOL = {"s": [0, 1, 2, 3], "v": [4, 5, 6], "m": [7]}
     turn = {"s": 0, "v": 0, "m": 0}
 
     def nextbank(k):
-        pool = {"s": SP, "v": VP, "m": MP}[k]
         turn[k] += 1
-        return pool[(turn[k] - 1) % len(pool)]
+        return POOL[k][(turn[k] - 1) % len(POOL[k])]
 
     ALL = [(s, b) for s in range(7) for b in range(4)]
     DWK = [["dw%d_%d%s" % (b, s, h) for s in range(7) for h in "le"] for b in range(4)]
@@ -255,11 +257,10 @@ def rank_program(g, core, T, topo):
     def slot(e, k, sig, b, halves):
         lo, hi = (0 if "l" in halves else 128), (256 if "e" in halves else 128)
         n = hi - lo
-        off = 16 * sig if sig % 2 == 0 else 224 + 16 * (sig - 1)
+        off = (16 * sig if sig % 2 == 0 else 224 + 16 * (sig - 1)) + 416 * b
         bk = nextbank(e)
         names = ["dw%d_%d%s" % (b, sig, h) for h in halves]
         q, s = T["xq%d" % k], T["xs%d" % k]
-        off += 416 * b
         mm(bk, n, T.ec[:, off:off + 128], T.es[:, off:off + 128], q[:, lo:hi], s[:, lo:hi],
            ["ec%d" % b] + ["xq%d%s" % (k, h) for h in halves])
 
@@ -271,140 +272,193 @@ def rank_program(g, core, T, topo):
                 act(out, bank(bk, n), ("b%d" % bk,), names)
         return copy
 
+    def windows(k, halves, todo):
+        todo, pending = list(todo), []
+
+        def advance():
+            while todo:
+                e, s, b = todo[0]
+                if e == "v":
+                    if len(pending) >= len(POOL["v"]):
+                        return
+                    pending.append(slot("v", k, s, b, halves))
+                else:
+                    slot("s", k, s, b, halves)()
+                todo.pop(0)
+
+        def fill():
+            if pending:
+                pending.pop(0)()
+                advance()
+
+        def flush():
+            while pending:
+                fill()
+        return advance, fill, flush
+
+    def deal(nv, skip=0):
+        rest, n = ALL[skip:], len(ALL) - skip
+        return [("v" if i * nv // n != (i + 1) * nv // n else "s", s, b) for i, (s, b) in enumerate(rest)]
+
     def scores(k, h):
         lo = 0 if h == "l" else 128
         bk = nextbank("m")
         mm(bk, 128, T["xq%d" % k][:, lo:lo + 128], T["xs%d" % k][:, lo:lo + 128], T.uq2[:], T.us2[:], ("xq%d%s" % (k, h), "uq2", "us2"))
         i = 0 if h == "l" else 1
-        return lambda: ts(T.bt[:, i:160:4], bank(bk, 40), 0.0, A.is_gt, ("b%d" % bk,), ("bt%d" % i,))
+        ts(T.bt[:, i:160:4], bank(bk, 40), 0.0, A.is_gt, ("b%d" % bk,), ("bt%d" % i,))
 
-    def lists(hf, dst):
-        m = slice(8 * hf, 8 * hf + 8)
-        ts(T.a0[:], T.t1[:, m], T.cs[:, 7:8], A.min, ("t1", "cs"), ("a0",), T.cs[:, 15:16], A.max)
-        tt(T.a1[:], T.c1[:, m], T.a0[:], A.subtract, ("c1", "a0"), ("a1",))
+    def counts(t, fill):
+        quant(T.bq[:], T.bs[:], T.bt[:], ("bt0", "bt1"), ("bq",))
+        bc = nextbank("m")
+        mm(bc, 128, T.onc[:], T.ons[:], T.bq[:], T.bs[:], ("on", "bq"))
+        fill()
+        fill()
+        fill()
+        tt(T.cp[:], bank(bc, 40), T.cm[:], A.mult, ("b%d" % bc, "cm0", "cm1", "cm2", "cm3", "cm4"), ("cp",))
+        vcopy(T.acs[:, t:24:3], bank(bc, 8), ("b%d" % bc,), ("acs",))
+        scan(T.cs[:], T.r8[:], T.cp[:], ("r8", "cp"), ("cs",))
+        fill()
+
+    def lists(fill):
+        ts(T.a0[:], T.t1[:], T.cs[:, 7:8], A.min, ("t1", "cs"), ("a0",), T.cs[:, 15:16], A.max)
+        fill()
+        tt(T.a1[:], T.c1[:], T.a0[:], A.subtract, ("c1", "a0"), ("a1",))
+        fill()
         vcopy(T.l1[:], T.a1[:], ("a1",), ("l1",))
-        tt(T.kg[:], T.w1[:, 0:3072].indirect(T.l1[:]), T.mk[:, 0:128], A.mult, ("w1", "po", "l1", "mk"), ("kg",))
-        scan(T.ks[:], T.rs[:, 0:128], T.kg[:], ("rs", "kg"), ("ks",))
-        v = T.ks[:, 15:128:16]
+        fill()
+        tt(T.kg[:], T.w1[:, 0:3072].indirect(T.l1[:]), T.mk[:], A.mult, ["w1", "w1_a", "w1_b", "l1", "mk"] + PO, ("kg",))
+        fill()
+        scan(T.ks[:], T.rs[:], T.kg[:], ("rs", "kg"), ("ks",))
+        fill()
+        v = T.ks[:, 15:256:16]
         ts(T.x1[:], v, 1920.0, A.is_lt, ("ks", "cs"), ("x1",), T.cs[:, 23:24], A.mult)
         ts(T.x2[:], v, 1280.0, A.is_lt, ("ks", "cs"), ("x2",), T.cs[:, 31:32], A.mult)
         ts(T.x3[:], v, 640.0, A.is_lt, ("ks", "cs"), ("x3",), T.cs[:, 39:40], A.mult)
         tt(T.x4[:], v, T.x1[:], A.subtract, ("ks", "x1"), ("x4",))
         tt(T.x5[:], T.x2[:], T.x3[:], A.add, ("x2", "x3"), ("x5",))
+        fill()
         tt(T.x6[:], T.x4[:], T.x5[:], A.subtract, ("x4", "x5"), ("x6",))
+        fill()
         vcopy(T.l2[:], T.x6[:], ("x6",), ("l2",))
-        tt(T.fg[:], T.ew[:, 0:2432].indirect(T.l2[:]), T.mk[:, 0:128], A.mult, ("ew", "ew_a", "ew_b", "ew0", "ew1", "ew2", "l2", "mk"), ("fg",))
-        scan(T.fs[:], T.rs[:, 0:128], T.fg[:], ("rs", "fg"), ("fs",))
-        vcopy(T[dst][:], T.fs[:, 15:128:16], ("fs",), (dst,))
+        fill()
+        tt(T.fg[:], T.ew[:, 0:2432].indirect(T.l2[:]), T.mk[:], A.mult, ["ew_a", "ew_b", "l2", "mk"] + ["ew%d%s" % (r, c) for r in range(3) for c in "xy"], ("fg",))
+        fill()
+        scan(T.fs[:], T.rs[:], T.fg[:], ("rs", "fg"), ("fs",))
+        fill()
+        vcopy(T.l3[:], T.fs[:, 15:256:16], ("fs",), ("l3",))
 
-    def gather(buf, dst):
+    def gather(buf, half):
         for b in range(4):
-            out, src = T[buf][:, b:512:4], T["dw%d" % b][:, 0:1792].indirect(T[dst][:])
-            if b % 2:
-                act(out, src, DWK[b] + [dst], ("%s_%d" % (buf, b),))
-            else:
-                vcopy(out, src, DWK[b] + [dst], ("%s_%d" % (buf, b),))
+            out, src = T[buf][:, b:512:4], T["dw%d" % b][:, 0:1792].indirect(T.l3[:, 8 * half:8 * half + 8])
+            (act if b % 2 else vcopy)(out, src, DWK[b] + ["l3"], ("%s_%d" % (buf, b),))
 
-    def tables():
-        for r, c in enumerate((0, 40, 80)):
-            op("v", lambda q, r=r, c=c: q.tensor_copy(T.w1[:, 1280:3072].indirect(T.ru[:, c:c + 20]), T.io2[:, 640 * r + 320:640 * r + 640]),
-               ("ru", "io2", "io3"), ("po",))
-        act(T.w1[:, 320:640], T.w1[:, 1280:3072].indirect(T.ru[:, 20:40]), ("po", "ru"), ("w1",))
-        act(T.k2[:], T.w1[:, 1280:3072].indirect(T.ru[:, 60:80]), ("po", "ru"), ("k2",))
-        op("v", lambda q: q.tensor_copy(T.pe[:].indirect(T.ru[:, 20:40]), T.io2[:, 320:640]), ("ru", "io2"), ("pe",))
-        op("v", lambda q: q.tensor_copy(T.pe[:].indirect(T.ru[:, 60:80]), T.iv[:]), ("ru", "iv"), ("pe",))
-        ts(T.vu[:], T.vi[:], T.kf[:, 0:1], A.subtract, ("vi", "kf"), ("vu",))
-        act(T.w1[:, 0:320], T.w1[:, 320:640], ("w1",), ("w1",))
-        act(T.w1[:, 640:1280], T.k2[:].indirect(T.vu[:]), ("k2", "vu"), ("w1",))
-        for r in range(3):
-            op("v", lambda q, r=r: q.transpose(T.ew[:, 640 * r + 320:640 * r + 640], T.eg[:, 320 * r:320 * r + 320]), ("eg",), ("ew%d" % r,))
-            act(T.ew[:, 640 * r:640 * r + 320], T.ew[:, 640 * r + 320:640 * r + 640], ("ew%d" % r,), ("ew",))
-        ts(T.ou[:], T.oi[:], T.s2[:, 0:1], A.add, ("oi", "s2"), ("ou",))
-        ts(T.mk[:], T.nn[:], T.kf[:, 0:1], A.is_equal, ("nn", "kf"), ("mk",))
-        ts(T.rs[:], T.nn[:], 0.0, A.not_equal, ("nn",), ("rs",))
-        tt(T.xc[:], T.pe[:, 512:1024].indirect(T.ou[:]), T.mk[:], A.mult, ("pe", "ou", "mk"), ("xc",))
-        scan(T.xd[:], T.rs[:], T.xc[:], ("rs", "xc"), ("xd",))
-        vcopy(T.c1[:], T.xd[:, 15:256:16], ("xd",), ("c1",))
-        ts(T.z1[:], T.c1[:], 1280.0, A.is_lt, ("c1",), ("z1",), -4096.0, A.mult)
-        ts(T.z2[:], T.c1[:], 640.0, A.is_lt, ("c1",), ("z2",), 8192.0, A.mult)
-        tt(T.t1[:], T.z1[:], T.z2[:], A.add, ("z1", "z2"), ("t1",))
+    def put_positions(r):
+        c = 40 * r
+        op("v", lambda q: q.tensor_copy(T.w1[:, 1280:3072].indirect(T.ru[:, c:c + 20]), T.io2[:, 640 * r + 320:640 * r + 640]),
+           ("ru", "io2", "io3", "io4"), PO)
+
+    def put_entries(c, src):
+        op("v", lambda q: q.tensor_copy(T.pe[:].indirect(T.ru[:, c:c + 20]), src), ("ru", "io2", "io3", "iv"), ("pe",))
 
     def countmask():
-        ts(T.gj[:], T.gi[:], T.ha[:, 0:1], A.add, ("gi", "ha"), ("gj",))
-        ts(T.gk[:], T.gj[:], 7, A.bitwise_and, ("gj",), ("gk",))
         ts(T.r8[:], T.gi[:], 8.0, A.not_equal, ("gi",), ("r8",))
+        ts(T.gk[:], T.gj[:], 7, A.bitwise_and, ("gj",), ("gk",))
+        ts(T.rs[:], T.nn[:], 0.0, A.not_equal, ("nn",), ("rs",))
         ts(T.cm[:, 0:8], T.gk[:, 0:8], 0.0, A.is_equal, ("gk",), ("cm0",))
-        ts(T.cm[:, 8:16], T.gk[:, 8:16], 2.0, A.is_equal, ("gk",), ("cm1",), -1.0, A.mult)
         ts(T.cm[:, 16:24], T.gk[:, 16:24], 3.0, A.is_equal, ("gk",), ("cm2",))
         ts(T.ca[:], T.gk[:, 24:32], 1.0, A.is_equal, ("gk",), ("ca",))
         ts(T.cb[:], T.gk[:, 32:40], 7.0, A.is_equal, ("gk",), ("cb",))
+        ts(T.cm[:, 8:16], T.gk[:, 8:16], 2.0, A.is_equal, ("gk",), ("cm1",), -1.0, A.mult)
         tt(T.cm[:, 24:32], T.ca[:], T.cm[:, 16:24], A.subtract, ("ca", "cm2"), ("cm3",))
         tt(T.cm[:, 32:40], T.cb[:], T.ca[:], A.subtract, ("cb", "ca"), ("cm4",))
 
+    def first():
+        for s, b in ALL[:NS_TABLES]:
+            slot("s", 0, s, b, "le")()
+        put_positions(0)
+        quant(T.uq[:], T.us[:], T.ub[:], ("ub",), ("uq",))
+        put_entries(20, T.io2[:, 320:640])
+        op("v", lambda q: q.tensor_copy(T.uq2[:].bitcast(dt.uint32), T.uq[:].bitcast(dt.uint32).indirect(T.uu[:])), ("uq", "uu"), ("uq2",))
+        put_positions(1)
+        op("v", lambda q: q.tensor_copy(T.us2[:], T.us[:].indirect(T.uu[:])), ("uq", "uu"), ("us2",))
+        memset("bt", 0.0, ("bt0", "bt1"))
+        put_positions(2)
+        ts(T.vu[:], T.vi[:], T.kf[:, 0:1], A.subtract, ("vi", "kf"), ("vu",))
+        act(T.k2[:], T.w1[:, 1280:3072].indirect(T.ru[:, 60:80]), PO + ["ru"], ("k2",))
+        act(T.w1[:, 320:640], T.w1[:, 1280:3072].indirect(T.ru[:, 20:40]), PO + ["ru"], ("w1_a",))
+        act(T.w1[:, 640:1280], T.k2[:].indirect(T.vu[:]), ("k2", "vu"), ("w1_b",))
+        for r in range(3):
+            op("v", lambda q, r=r: q.transpose(T.ew[:, 640 * r + 320:640 * r + 640], T.eg[:, 320 * r:320 * r + 320]), ("eg",), ("ew%dx" % r,))
+        scores(0, "l")
+        put_entries(60, T.iv[:])
+        for r in range(3):
+            gcopy(T.ew[:, 640 * r:640 * r + 320], T.ew[:, 640 * r + 320:640 * r + 640], 320, ("ew%dx" % r,), ("ew%dy" % r,))
+        gcopy(T.w1[:, 0:320], T.w1[:, 320:640], 320, ("w1_a",), ("w1",))
+        scores(0, "e")
+        memset("ot", 1.0, ("ot",))
+        ts(T.gj[:], T.gi[:], T.ha[:, 0:1], A.add, ("gi", "ha"), ("gj",))
+        ts(T.mk[:], T.nn[:], T.kf[:, 0:1], A.is_equal, ("nn", "kf"), ("mk",))
+        ts(T.ou[:], T.oi[:], T.s2[:, 0:1], A.add, ("oi", "s2"), ("ou",))
+        quant(T.onc[:], T.ons[:], T.ot[:], ("ot",), ("on",))
+        countmask()
+        advance, fill, flush = windows(0, "le", deal(NV_R0, NS_TABLES))
+        advance()
+        tt(T.xc[:], T.pe[:, 512:1024].indirect(T.ou[:]), T.mk[:], A.mult, ("pe", "ou", "mk"), ("xc",))
+        counts(0, lambda: None)
+        scan(T.xd[:], T.rs[:], T.xc[:], ("rs", "xc"), ("xd",))
+        fill()
+        vcopy(T.c1[:], T.xd[:, 15:256:16], ("xd",), ("c1",))
+        fill()
+        ts(T.z1[:], T.c1[:], 1280.0, A.is_lt, ("c1",), ("z1",), -4096.0, A.mult)
+        ts(T.z2[:], T.c1[:], 640.0, A.is_lt, ("c1",), ("z2",), 8192.0, A.mult)
+        fill()
+        tt(T.t1[:], T.z1[:], T.z2[:], A.add, ("z1", "z2"), ("t1",))
+        lists(fill)
+        flush()
+
     for t in range(3):
-        k = t
-        is_late = scores(k, "l")
-        is_early = scores(k, "e") if t == 0 else None
-        halves = "le" if t == 0 else "l"
-        nv = NV_R0 if t == 0 else NV_LATE
-        first = [slot("v", k, s, b, halves) for s, b in ALL[:NV_FIRST]]
-        mids = [slot("s", k, s, b, halves) for s, b in ALL[NV_FIRST:NV_FIRST + 4]]
-        is_late()
-        if is_early:
-            is_early()
-        quant(T.bq[:], T.bs[:], T.bt[:], ("bt0", "bt1"), ("bq",))
-        bc = nextbank("m")
-        mm(bc, 128, T.onc[:], T.ons[:], T.bq[:], T.bs[:], ("on", "bq"))
-        for c in first:
-            c()
+        n = t + 1
         if t == 0:
-            countmask()
-        tt(T.cp[:], bank(bc, 40), T.cm[:], A.mult, ("b%d" % bc, "cm0", "cm1", "cm2", "cm3", "cm4"), ("cp",))
-        scan(T.cs[:], T.r8[:], T.cp[:], ("r8", "cp"), ("cs",))
-        vcopy(T.acs[:, t:24:3], bank(bc, 8), ("b%d" % bc,), ("acs",))
-        for c in mids:
-            c()
-        rest = ALL[NV_FIRST + 4:]
-        nrest = len(rest) - (nv - NV_FIRST)
-        for i, (s, b) in enumerate(rest[:nrest]):
-            if t == 0 and i == NS_TABLES:
-                tables()
-            slot("s", k, s, b, halves)()
-        lists(0, "l3")
-        for s, b in rest[nrest:]:
-            slot("v", k, s, b, halves)()
-        gather("gt", "l3")
+            first()
+        else:
+            advance, fill, flush = windows(t, "l", deal(NV_LATE))
+            scores(t, "l")
+            advance()
+            counts(t, fill)
+            lists(fill)
+            flush()
+        gather("gt", 0)
         w = slice(128 * t, 128 * t + 128)
         quant(T.gq[:, w], T.gs[:, w], T.gt[:], ["gt_%d" % b for b in range(4)], ("gq%d" % t,))
         addr = topo.addr(partner[t])
         send(T.rq[:, w].bitcast(dt.uint8), T.gq[:, w].bitcast(dt.uint8), "ar%d" % t, "lo%d" % t, addr, emask, engines, ("gq%d" % t,))
         send(T.rp[:, w], T.gs[:, w], "ar%d" % t, "lo%d" % t, addr, emask, engines, ("gq%d" % t,))
         landed("ar%d" % t, ("rq%d" % t,))
-        lists(1, "l4")
-        gather("yo", "l4")
+        gather("yo", 1)
         YO = ["yo_%d" % b for b in range(4)]
         quant(T.yq[:], T.yp[:], T.yo[:], YO, ("yq",))
-        n = k + 1
+        ts(T.y32[:], T.yo[:], 32.0, A.mult, YO, ("y32",))
         for b in range(4):
-            bk = nextbank("s")
+            bk = b
             mm(bk, 128, T.wq[:, 128 * b:128 * b + 128], T.wp[:, 128 * b:128 * b + 128], T.yq[:], T.yp[:], ("wq", "wp", "yq"))
-            act(T["tm%d" % b][:], bank(bk, 128), ("b%d" % bk,), ("tm%d" % b,), scale=0.03125)
-            tt(T.xt[:, 512 + b:1024:4], T["tm%d" % b][:], T.yo[:, b:512:4], A.add, ("tm%d" % b, YO[b]), ("xe%d" % b,))
-        quant(T["xq%d" % n][:, 128:256], T["xs%d" % n][:, 128:256], T.xt[:, 512:1024], ["xe%d" % b for b in range(4)], ("xq%de" % n,))
+            tt(T["tm%d" % b][:], bank(bk, 128), T.y32[:, b:512:4], A.add, ("b%d" % bk, "y32"), ("tm%d" % b,))
+            act(T.xt[:, 512 + b:1024:4], T["tm%d" % b][:], ("tm%d" % b,), ("xe%d" % b,), scale=0.03125)
         if t == 0:
-            op("v", lambda q: q.memset(T.it[:], 0.0), (), ("it",))
+            memset("it", 0.0, ("it",))
+        quant(T["xq%d" % n][:, 128:256], T["xs%d" % n][:, 128:256], T.xt[:, 512:1024], ["xe%d" % b for b in range(4)], ("xq%de" % n,))
+        if n < 3:
+            scores(n, "e")
+        if t == 0:
             ts(T.it[:, 3:515:4], T.ii[:], T.pf[:, 0:1], A.is_equal, ("ii", "pf"), ("it",))
             ts(T.it[:, 515:1027:4], T.ii[:], T.pf[:, 0:1], A.is_equal, ("ii", "pf"), ("it",), 32.0, A.mult)
             for b in range(4):
                 quant(T.ic[:, 256 * b:256 * b + 256], T.ip[:, 256 * b:256 * b + 256], T.it[:, 3 - b:1027 - b], ("it",), ("ic%d" % b,))
-            quant(T.vq[:], T.vs[:], T.vb[:], ("vb",), ("vq",))
         if n < 3:
-            scores(n, "e")()
-            for i, (s, b) in enumerate(ALL):
-                slot("v" if i * NV_EARLY // 28 != (i + 1) * NV_EARLY // 28 else "s", n, s, b, "e")()
+            for e, s, b in deal(NV_EARLY):
+                slot(e, n, s, b, "e")()
         else:
-            mm(6, 128, T.vq[:], T.vs[:], T.xq3[:, 128:256], T.xs3[:, 128:256], ("vq", "xq3e"))
-            vcopy(T.ys[:, 128:256], bank(6, 128), ("b6",), ("yse",))
+            mm(7, 128, T.vq[:], T.vs[:], T.xq3[:, 128:256], T.xs3[:, 128:256], ("vq", "xq3e"))
+            vcopy(T.ys[:, 128:256], bank(7, 128), ("b7",), ("yse",))
             dma("y", T.y[:, 128:256], T.ys[:, 128:256], "do", ("yse",), ())
             dma("y", T.oc[:, 512:1024], T.xq3[:, 128:256].bitcast(dt.uint8), "do", ("xq3e",), ())
             for i in range(4):
@@ -418,11 +472,10 @@ def rank_program(g, core, T, topo):
         for b in range(4):
             mm(rb[b], 128, T.ic[:, 256 * b + 128:256 * b + 256], T.ip[:, 256 * b + 128:256 * b + 256], rq, rp, ("ic%d" % b, "rq%d" % t), True, False)
         for b in range(4):
-            if b % 2:
-                vcopy(T.zl[:, b:512:4], bank(ub[b], 128), ("b%d" % ub[b],), ("zl%d" % b,))
-            else:
-                act(T.zl[:, b:512:4], bank(ub[b], 128), ("b%d" % ub[b],), ("zl%d" % b,))
+            (vcopy if b % 2 else act)(T.zl[:, b:512:4], bank(ub[b], 128), ("b%d" % ub[b],), ("zl%d" % b,))
         quant(T.zq[:], T.zp[:], T.zl[:], ["zl%d" % b for b in range(4)], ("zq",))
+        if t == 1:
+            quant(T.vq[:], T.vs[:], T.vb[:], ("vb",), ("vq",))
         for b in range(4):
             mm(rb[b], 128, T.wq[:, 128 * b:128 * b + 128], T.wp[:, 128 * b:128 * b + 128], T.zq[:], T.zp[:], ("wq", "wp", "zq"), False, True)
         for b in range(4):

@@ -1,8 +1,9 @@
 from concourse.mybir import dt, AluOpType as A, ActivationFunctionType as F
 
 MASKS = [1, 2, 4]
-NV_LATE, NV_EARLY = 12, 14
-NV_R0, NS_TABLES = 6, 12
+NV_LATE, NV_EARLY = 3, 12
+NS_MORE, NS_COUNT = 10, 3
+NV_R0, NS_TABLES = 0, 4
 
 F32, BF, I32, U16, U8, MXW = "float32", "bfloat16", "int32", "uint16", "uint8", "float8_e4m3fn_x4"
 
@@ -21,14 +22,14 @@ SCRATCH = {
     "pi": _sb(1, I32), "pa": _sb(1, I32), "pb": _sb(1, I32), "pk": _sb(1, I32),
     "pf": _sb(1, F32), "mo": _sb(1, F32), "me": _sb(1, F32), "fr": _sb(1, F32), "kf": _sb(1, F32),
     "ha": _sb(1, F32), "s2": _sb(1, F32),
-    "nn": _sb(256, I32), "mk": _sb(256, F32), "rs": _sb(256, F32),
-    "gi": _sb(40, I32), "gj": _sb(40, I32), "gk": _sb(40, I32), "cm": _sb(40, F32), "ca": _sb(8, F32), "cb": _sb(8, F32), "r8": _sb(40, F32),
+    "nn": _sb(256, F32), "mk": _sb(256, F32), "rs": _sb(256, F32),
+    "gi": _sb(80, I32), "gj": _sb(80, I32), "gk": _sb(80, I32), "ge": _sb(80, F32), "cm": _sb(40, F32), "g8": _sb(40, F32), "r8": _sb(40, F32),
     "li": _sb(60, I32), "lu": _sb(60, U16), "vi": _sb(40, I32), "vu": _sb(40, U16),
     "oi": _sb(16, I32), "ou": _sb(16, U16), "ui": _sb(8, I32), "uj": _sb(8, I32), "uu": _sb(8, U16),
     "onc": _sb(128, MXW), "ons": _sb(128, U8), "bq": _sb(128, MXW), "bs": _sb(128, U8),
     "ra": _sb(100, I32), "rb": _sb(100, I32), "rc": _sb(100, I32), "rd": _sb(100, I32),
     "ru": _sb(100, U16), "rf": _sb(100, F32), "eg": _sb(960, F32),
-    "io2": _sb(1920, F32), "iv": _sb(320, F32), "ew": _sb(2432, F32), "w1": _sb(3072, F32),
+    "io2": _sb(1920, F32), "iv": _sb(320, F32), "ew": _sb(2816, F32), "w1": _sb(2560, F32),
     "pe": _sb(1792, F32), "k2": _sb(320, F32), "xc": _sb(256, F32), "xd": _sb(256, F32),
     "c1": _sb(16, F32), "t1": _sb(16, F32), "z1": _sb(16, F32), "z2": _sb(16, F32),
     "cp": _sb(40, F32), "cs": _sb(40, F32), "acs": _sb(24, F32),
@@ -48,7 +49,7 @@ for _n, _d in (("gq", MXW), ("gs", U8), ("rq", MXW), ("rp", U8)):
 for _n, _w, _d in (("ec", 1664, MXW), ("es", 1664, U8), ("ic", 1024, MXW), ("ip", 1024, U8)):
     SCRATCH[_n] = _sb(_w, _d)
 
-SEMAPHORES = ["cv", "cs", "ct", "cg", "dr", "dx", "du", "dv", "dw", "do", "dp"] + ["ar%d" % t for t in range(3)] + ["lo%d" % t for t in range(3)]
+SEMAPHORES = ["cv", "cs", "ct", "cg", "dr", "dx", "du", "dv", "dw", "dk", "do", "dp"] + ["ar%d" % t for t in range(3)] + ["lo%d" % t for t in range(3)]
 
 
 def _tracker(g, T):
@@ -154,13 +155,13 @@ def rank_program(g, core, T, topo):
     def vcopy(out, in_, rd, wr):
         op("v", lambda q: q.tensor_copy(out, in_), rd, wr)
 
-    def act(out, in_, rd, wr, bias=None, scale=None):
+    def act(out, in_, rd, wr, bias=None, scale=None, func=F.Copy):
         if bias is None and scale is None:
-            op("s", lambda q: q.activation(out, in_, COPY), rd, wr)
+            op("s", lambda q: q.activation(out, in_, func), rd, wr)
         elif bias is None:
             op("s", lambda q: q.activation(out, in_, COPY, scale=scale), rd, wr)
         else:
-            op("s", lambda q: q.activation(out, in_, IDENT, bias=bias, scale=1.0), rd, wr)
+            op("s", lambda q: q.activation(out, in_, IDENT, bias=bias, scale=1.0 if scale is None else scale), rd, wr)
 
     def quant(out, sc, in_, rd, wr):
         op("v", lambda q: q.quantize_mx(out, sc, in_), rd, wr)
@@ -199,10 +200,14 @@ def rank_program(g, core, T, topo):
     iota("li", 0, 60, [[40, 3], [2, 10], [0, 2]], 0, 0)
     iota("ui", 0, 8, [[0, 8]], 0, 16)
     iota("iv", 0, 320, [[-1, 320]], 959, 0, True)
-    iota("nn", 0, 256, [[0, 16], [1, 16]], 0, 0)
-    iota("gi", 0, 40, [[0, 5], [1, 8]], 8, 0)
-    iota("oi", 0, 16, [[16, 16]], 0, 0)
+    iota("nn", 0, 256, [[0, 16], [1, 16]], 0, 0, True)
     iota("vi", 0, 40, [[0, 2], [-16, 20]], 319, 0)
+    iota("g8", 0, 40, [[0, 5], [1, 8]], 0, 0, True)
+    GI = ["gi%d" % i for i in range(10)]
+    for i, d in enumerate((0, None, 3, 1, 7, None, 2, None, 3, 1)):
+        iota("gi", 8 * i, 8 * i + 8, [[8, 8]] if d is None else [[1, 8]], 9 if d is None else 8 - d, 0, key=GI[i])
+    iota("oi", 0, 16, [[16, 16]], 0, 0)
+    iota("ew", 2176, 2560, [[1, 384]], 0, 0, True, key="ew_c")
     iota("ii", 0, 128, [[1, 128]], 0, 0)
 
     memset("et", 0.0, ("et",))
@@ -234,15 +239,15 @@ def rank_program(g, core, T, topo):
     act(T.io2[:, 480:960], T.io2[:, 0:480], ("io2",), ("io3",), bias=480.0)
     act(T.w1[:, 1280:1792], T.io2[:, 0:512], ("io2", "io3"), ("po_a",))
     act(T.w1[:, 1792:2048], T.io2[:, 0:256], ("io2",), ("po_b",), bias=1920.0)
-    act(T.w1[:, 2048:2304], T.io2[:, 0:256], ("io2",), ("po_c",))
-    act(T.w1[:, 2304:2560], T.io2[:, 0:256], ("io2",), ("po_d",), bias=2176.0)
-    act(T.w1[:, 2560:3072], T.io2[:, 0:512], ("io2", "io3"), ("po_e",))
-    act(T.io2[:, 960:1920], T.io2[:, 0:960], ("io2", "io3"), ("io4",), bias=960.0)
+    act(T.w1[:, 2048:2560], T.io2[:, 0:512], ("io2", "io3"), ("po_c",))
+    act(T.io2[:, 960:1280], T.io2[:, 0:320], ("io2",), ("io4",), bias=960.0)
     act(T.pe[:, 512:1024], T.io2[:, 512:1024], ("io3", "io4"), ("pe",), bias=1280.0)
     act(T.ew[:, 1920:2176], T.io2[:, 512:768], ("io3",), ("ew_a",))
-    act(T.ew[:, 2176:2432], T.io2[:, 1024:1280], ("io4",), ("ew_b",))
+    act(T.ew[:, 2560:2816], T.io2[:, 1024:1280], ("io4",), ("ew_b",))
     act(T.eg[:], T.rf[:].indirect(T.lu[:]), ("rf", "lu"), ("eg",))
-    PO = ["po", "po_a", "po_b", "po_c", "po_d", "po_e"]
+    act(T.bt[:], T.io2[:, 0:512], ("io2", "io3"), ("bt0", "bt1"), scale=0.0)
+    act(T.ot[:], T.io2[:, 0:512], ("io2", "io3"), ("ot",), bias=1.0, scale=0.0)
+    PO = ["po", "po_a", "po_b", "po_c"]
 
     POOL = {"s": [0, 1, 2, 3], "v": [4, 5, 6], "m": [7]}
     turn = {"s": 0, "v": 0, "m": 0}
@@ -275,8 +280,9 @@ def rank_program(g, core, T, topo):
     def windows(k, halves, todo):
         todo, pending = list(todo), []
 
-        def advance():
-            while todo:
+        def advance(most=99):
+            while todo and most:
+                most -= 1
                 e, s, b = todo[0]
                 if e == "v":
                     if len(pending) >= len(POOL["v"]):
@@ -296,7 +302,9 @@ def rank_program(g, core, T, topo):
                 fill()
         return advance, fill, flush
 
-    def deal(nv, skip=0):
+    def deal(nv, skip=0, lead=0):
+        if lead:
+            return [("v", s, b) for s, b in ALL[:lead]] + deal(nv - lead, lead)
         rest, n = ALL[skip:], len(ALL) - skip
         return [("v" if i * nv // n != (i + 1) * nv // n else "s", s, b) for i, (s, b) in enumerate(rest)]
 
@@ -307,70 +315,80 @@ def rank_program(g, core, T, topo):
         i = 0 if h == "l" else 1
         ts(T.bt[:, i:160:4], bank(bk, 40), 0.0, A.is_gt, ("b%d" % bk,), ("bt%d" % i,))
 
-    def counts(t, fill):
+    def counts(t, fill, advance):
         quant(T.bq[:], T.bs[:], T.bt[:], ("bt0", "bt1"), ("bq",))
         bc = nextbank("m")
         mm(bc, 128, T.onc[:], T.ons[:], T.bq[:], T.bs[:], ("on", "bq"))
+        advance()
         fill()
         fill()
         fill()
-        tt(T.cp[:], bank(bc, 40), T.cm[:], A.mult, ("b%d" % bc, "cm0", "cm1", "cm2", "cm3", "cm4"), ("cp",))
+        tt(T.cp[:], bank(bc, 40), T.cm[:], A.mult, ("b%d" % bc, "cm"), ("cp",))
         vcopy(T.acs[:, t:24:3], bank(bc, 8), ("b%d" % bc,), ("acs",))
         scan(T.cs[:], T.r8[:], T.cp[:], ("r8", "cp"), ("cs",))
         fill()
 
+    def chain(h):
+        m, w = slice(8 * h, 8 * h + 8), slice(128 * h, 128 * h + 128)
+        mk, rs, v, f = T.mk[:, 0:128], T.rs[:, 0:128], T.ks[:, 128 * h + 15:128 * h + 128:16], T.fs[:, 128 * h + 15:128 * h + 128:16]
+        k = {n: "%s_%d" % (n, h) for n in ("a0", "a1", "l1", "kg", "ks", "x1", "x2", "x3", "x4", "x5", "x6", "l2", "fg", "fs", "l3")}
+        ts(T.a0[:, m], T.t1[:, m], T.cs[:, 7:8], A.min, ("t1", "cs"), (k["a0"],), T.cs[:, 15:16], A.max)
+        yield
+        tt(T.a1[:, m], T.c1[:, m], T.a0[:, m], A.subtract, ("c1", k["a0"]), (k["a1"],))
+        yield
+        vcopy(T.l1[:, m], T.a1[:, m], (k["a1"],), (k["l1"],))
+        yield
+        tt(T.kg[:, w], T.w1[:].indirect(T.l1[:, m]), mk, A.mult, ["w1", "w1_a", "w1_b", k["l1"], "mk"] + PO, (k["kg"],))
+        yield
+        scan(T.ks[:, w], rs, T.kg[:, w], ("rs", k["kg"]), (k["ks"],))
+        yield
+        ts(T.x1[:, m], v, 1920.0, A.is_lt, (k["ks"], "cs"), (k["x1"],), T.cs[:, 23:24], A.mult)
+        ts(T.x2[:, m], v, 1280.0, A.is_lt, (k["ks"], "cs"), (k["x2"],), T.cs[:, 31:32], A.mult)
+        ts(T.x3[:, m], v, 640.0, A.is_lt, (k["ks"], "cs"), (k["x3"],), T.cs[:, 39:40], A.mult)
+        yield
+        tt(T.x4[:, m], v, T.x1[:, m], A.subtract, (k["ks"], k["x1"]), (k["x4"],))
+        tt(T.x5[:, m], T.x2[:, m], T.x3[:, m], A.add, (k["x2"], k["x3"]), (k["x5"],))
+        yield
+        tt(T.x6[:, m], T.x4[:, m], T.x5[:, m], A.subtract, (k["x4"], k["x5"]), (k["x6"],))
+        yield
+        vcopy(T.l2[:, m], T.x6[:, m], (k["x6"],), (k["l2"],))
+        yield
+        tt(T.fg[:, w], T.ew[:].indirect(T.l2[:, m]), mk, A.mult,
+           ["ew_a", "ew_b", "ew_c", k["l2"], "mk"] + ["ew%d%s" % (r, c) for r in range(3) for c in "xy"], (k["fg"],))
+        yield
+        scan(T.fs[:, w], rs, T.fg[:, w], ("rs", k["fg"]), (k["fs"],))
+        yield
+        vcopy(T.l3[:, m], f, (k["fs"],), (k["l3"],))
+
     def lists(fill):
-        ts(T.a0[:], T.t1[:], T.cs[:, 7:8], A.min, ("t1", "cs"), ("a0",), T.cs[:, 15:16], A.max)
-        fill()
-        tt(T.a1[:], T.c1[:], T.a0[:], A.subtract, ("c1", "a0"), ("a1",))
-        fill()
-        vcopy(T.l1[:], T.a1[:], ("a1",), ("l1",))
-        fill()
-        tt(T.kg[:], T.w1[:, 0:3072].indirect(T.l1[:]), T.mk[:], A.mult, ["w1", "w1_a", "w1_b", "l1", "mk"] + PO, ("kg",))
-        fill()
-        scan(T.ks[:], T.rs[:], T.kg[:], ("rs", "kg"), ("ks",))
-        fill()
-        v = T.ks[:, 15:256:16]
-        ts(T.x1[:], v, 1920.0, A.is_lt, ("ks", "cs"), ("x1",), T.cs[:, 23:24], A.mult)
-        ts(T.x2[:], v, 1280.0, A.is_lt, ("ks", "cs"), ("x2",), T.cs[:, 31:32], A.mult)
-        ts(T.x3[:], v, 640.0, A.is_lt, ("ks", "cs"), ("x3",), T.cs[:, 39:40], A.mult)
-        tt(T.x4[:], v, T.x1[:], A.subtract, ("ks", "x1"), ("x4",))
-        tt(T.x5[:], T.x2[:], T.x3[:], A.add, ("x2", "x3"), ("x5",))
-        fill()
-        tt(T.x6[:], T.x4[:], T.x5[:], A.subtract, ("x4", "x5"), ("x6",))
-        fill()
-        vcopy(T.l2[:], T.x6[:], ("x6",), ("l2",))
-        fill()
-        tt(T.fg[:], T.ew[:, 0:2432].indirect(T.l2[:]), T.mk[:], A.mult, ["ew_a", "ew_b", "l2", "mk"] + ["ew%d%s" % (r, c) for r in range(3) for c in "xy"], ("fg",))
-        fill()
-        scan(T.fs[:], T.rs[:], T.fg[:], ("rs", "fg"), ("fs",))
-        fill()
-        vcopy(T.l3[:], T.fs[:, 15:256:16], ("fs",), ("l3",))
+        second = chain(1)
+        for _ in chain(0):
+            next(second, None)
+            fill()
+        return second
 
     def gather(buf, half):
         for b in range(4):
             out, src = T[buf][:, b:512:4], T["dw%d" % b][:, 0:1792].indirect(T.l3[:, 8 * half:8 * half + 8])
-            (act if b % 2 else vcopy)(out, src, DWK[b] + ["l3"], ("%s_%d" % (buf, b),))
+            (act if b % 2 else vcopy)(out, src, DWK[b] + ["l3_%d" % half], ("%s_%d" % (buf, b),))
 
     def put_positions(r):
         c = 40 * r
-        op("v", lambda q: q.tensor_copy(T.w1[:, 1280:3072].indirect(T.ru[:, c:c + 20]), T.io2[:, 640 * r + 320:640 * r + 640]),
+        op("v", lambda q: q.tensor_copy(T.w1[:, 1280:2560].indirect(T.ru[:, c:c + 20]), T.io2[:, 640 * r + 320:640 * r + 640]),
            ("ru", "io2", "io3", "io4"), PO)
 
     def put_entries(c, src):
         op("v", lambda q: q.tensor_copy(T.pe[:].indirect(T.ru[:, c:c + 20]), src), ("ru", "io2", "io3", "iv"), ("pe",))
 
     def countmask():
-        ts(T.r8[:], T.gi[:], 8.0, A.not_equal, ("gi",), ("r8",))
+        ts(T.gj[:], T.gi[:], T.ha[:, 0:1], A.add, GI + ["ha"], ("gj",))
+        ts(T.mk[:], T.nn[:], T.kf[:, 0:1], A.is_equal, ("nn", "kf"), ("mk",))
         ts(T.gk[:], T.gj[:], 7, A.bitwise_and, ("gj",), ("gk",))
-        ts(T.rs[:], T.nn[:], 0.0, A.not_equal, ("nn",), ("rs",))
-        ts(T.cm[:, 0:8], T.gk[:, 0:8], 0.0, A.is_equal, ("gk",), ("cm0",))
-        ts(T.cm[:, 16:24], T.gk[:, 16:24], 3.0, A.is_equal, ("gk",), ("cm2",))
-        ts(T.ca[:], T.gk[:, 24:32], 1.0, A.is_equal, ("gk",), ("ca",))
-        ts(T.cb[:], T.gk[:, 32:40], 7.0, A.is_equal, ("gk",), ("cb",))
-        ts(T.cm[:, 8:16], T.gk[:, 8:16], 2.0, A.is_equal, ("gk",), ("cm1",), -1.0, A.mult)
-        tt(T.cm[:, 24:32], T.ca[:], T.cm[:, 16:24], A.subtract, ("ca", "cm2"), ("cm3",))
-        tt(T.cm[:, 32:40], T.cb[:], T.ca[:], A.subtract, ("cb", "ca"), ("cm4",))
+        ts(T.ou[:], T.oi[:], T.s2[:, 0:1], A.add, ("oi", "s2"), ("ou",))
+        quant(T.onc[:], T.ons[:], T.ot[:], ("ot",), ("on",))
+        ts(T.ge[:], T.gk[:], 0.0, A.is_equal, ("gk",), ("ge",))
+        tt(T.xc[:], T.pe[:, 512:1024].indirect(T.ou[:]), T.mk[:], A.mult, ("pe", "ou", "mk"), ("xc",))
+        tt(T.cm[:], T.ge[:, 0:40], T.ge[:, 40:80], A.subtract, ("ge",), ("cm",))
 
     def first():
         for s, b in ALL[:NS_TABLES]:
@@ -381,12 +399,12 @@ def rank_program(g, core, T, topo):
         op("v", lambda q: q.tensor_copy(T.uq2[:].bitcast(dt.uint32), T.uq[:].bitcast(dt.uint32).indirect(T.uu[:])), ("uq", "uu"), ("uq2",))
         put_positions(1)
         op("v", lambda q: q.tensor_copy(T.us2[:], T.us[:].indirect(T.uu[:])), ("uq", "uu"), ("us2",))
-        memset("bt", 0.0, ("bt0", "bt1"))
-        put_positions(2)
         ts(T.vu[:], T.vi[:], T.kf[:, 0:1], A.subtract, ("vi", "kf"), ("vu",))
-        act(T.k2[:], T.w1[:, 1280:3072].indirect(T.ru[:, 60:80]), PO + ["ru"], ("k2",))
-        act(T.w1[:, 320:640], T.w1[:, 1280:3072].indirect(T.ru[:, 20:40]), PO + ["ru"], ("w1_a",))
-        act(T.w1[:, 640:1280], T.k2[:].indirect(T.vu[:]), ("k2", "vu"), ("w1_b",))
+        act(T.w1[:, 320:640], T.w1[:, 1280:2560].indirect(T.ru[:, 20:40]), PO + ["ru"], ("w1_a",))
+        dma("y", T.k2[0:96, :], T.w1[32:128, 320:640], "dk", ("w1_a",), ("k2",))
+        dma("y", T.k2[96:128, :], T.w1[0:32, 320:640], "dk", ("w1_a",), ("k2_",))
+        act(T.rs[:], T.nn[:], ("nn",), ("rs",), func=F.Sign)
+        act(T.r8[:], T.g8[:], ("g8",), ("r8",), func=F.Sign)
         for r in range(3):
             op("v", lambda q, r=r: q.transpose(T.ew[:, 640 * r + 320:640 * r + 640], T.eg[:, 320 * r:320 * r + 320]), ("eg",), ("ew%dx" % r,))
         scores(0, "l")
@@ -395,17 +413,13 @@ def rank_program(g, core, T, topo):
             gcopy(T.ew[:, 640 * r:640 * r + 320], T.ew[:, 640 * r + 320:640 * r + 640], 320, ("ew%dx" % r,), ("ew%dy" % r,))
         gcopy(T.w1[:, 0:320], T.w1[:, 320:640], 320, ("w1_a",), ("w1",))
         scores(0, "e")
-        memset("ot", 1.0, ("ot",))
-        ts(T.gj[:], T.gi[:], T.ha[:, 0:1], A.add, ("gi", "ha"), ("gj",))
-        ts(T.mk[:], T.nn[:], T.kf[:, 0:1], A.is_equal, ("nn", "kf"), ("mk",))
-        ts(T.ou[:], T.oi[:], T.s2[:, 0:1], A.add, ("oi", "s2"), ("ou",))
-        quant(T.onc[:], T.ons[:], T.ot[:], ("ot",), ("on",))
         countmask()
-        advance, fill, flush = windows(0, "le", deal(NV_R0, NS_TABLES))
-        advance()
-        tt(T.xc[:], T.pe[:, 512:1024].indirect(T.ou[:]), T.mk[:], A.mult, ("pe", "ou", "mk"), ("xc",))
-        counts(0, lambda: None)
+        advance, fill, flush = windows(0, "le", deal(NV_R0, NS_TABLES + NS_MORE))
+        for s, b in ALL[NS_TABLES:NS_TABLES + NS_MORE]:
+            slot("s", 0, s, b, "le")()
+        act(T.w1[:, 640:1280], T.k2[:].indirect(T.vu[:]), ("k2", "k2_", "vu"), ("w1_b",), bias=640.0)
         scan(T.xd[:], T.rs[:], T.xc[:], ("rs", "xc"), ("xd",))
+        counts(0, lambda: None, advance)
         fill()
         vcopy(T.c1[:], T.xd[:, 15:256:16], ("xd",), ("c1",))
         fill()
@@ -413,21 +427,23 @@ def rank_program(g, core, T, topo):
         ts(T.z2[:], T.c1[:], 640.0, A.is_lt, ("c1",), ("z2",), 8192.0, A.mult)
         fill()
         tt(T.t1[:], T.z1[:], T.z2[:], A.add, ("z1", "z2"), ("t1",))
-        lists(fill)
+        second = lists(fill)
         flush()
+        return second
 
     for t in range(3):
         n = t + 1
         if t == 0:
-            first()
+            second = first()
         else:
-            advance, fill, flush = windows(t, "l", deal(NV_LATE))
+            advance, fill, flush = windows(t, "l", deal(NV_LATE, 0, 3))
             scores(t, "l")
-            advance()
-            counts(t, fill)
-            lists(fill)
+            advance(3 + NS_COUNT)
+            counts(t, fill, advance)
+            second = lists(fill)
             flush()
         gather("gt", 0)
+        next(second, None)
         w = slice(128 * t, 128 * t + 128)
         quant(T.gq[:, w], T.gs[:, w], T.gt[:], ["gt_%d" % b for b in range(4)], ("gq%d" % t,))
         addr = topo.addr(partner[t])

from concourse.mybir import dt, AluOpType as A, ActivationFunctionType as F

MASKS = [1, 2, 4]
NV_LATE, NV_EARLY = 3, 12
NS_MORE, NS_COUNT = 10, 3
NV_R0, NS_TABLES = 0, 4

F32, BF, I32, U16, U8, MXW = "float32", "bfloat16", "int32", "uint16", "uint8", "float8_e4m3fn_x4"


def _sb(n, d):
    return ("sbuf", [128, n], d)


SCRATCH = {
    "ps": ("psum", [128, 4096], F32),
    "xb": _sb(1024, BF), "ub": _sb(512, BF), "vb": _sb(512, BF), "rl": _sb(120, I32),
    "uq": _sb(128, MXW), "us": _sb(128, U8), "uq2": _sb(128, MXW), "us2": _sb(128, U8),
    "vq": _sb(128, MXW), "vs": _sb(128, U8), "wq": _sb(512, MXW), "wp": _sb(512, U8),
    "et": _sb(1668, BF), "it": _sb(1028, BF), "ot": _sb(512, BF), "bt": _sb(512, BF),
    "ci": _sb(416, I32), "cj": _sb(416, I32), "ii": _sb(128, I32),
    "pi": _sb(1, I32), "pa": _sb(1, I32), "pb": _sb(1, I32), "pk": _sb(1, I32),
    "pf": _sb(1, F32), "mo": _sb(1, F32), "me": _sb(1, F32), "fr": _sb(1, F32), "kf": _sb(1, F32),
    "ha": _sb(1, F32), "s2": _sb(1, F32),
    "nn": _sb(256, F32), "mk": _sb(256, F32), "rs": _sb(256, F32),
    "gi": _sb(80, I32), "gj": _sb(80, I32), "gk": _sb(80, I32), "ge": _sb(80, F32), "cm": _sb(40, F32), "g8": _sb(40, F32), "r8": _sb(40, F32),
    "li": _sb(60, I32), "lu": _sb(60, U16), "vi": _sb(40, I32), "vu": _sb(40, U16),
    "oi": _sb(16, I32), "ou": _sb(16, U16), "ui": _sb(8, I32), "uj": _sb(8, I32), "uu": _sb(8, U16),
    "onc": _sb(128, MXW), "ons": _sb(128, U8), "bq": _sb(128, MXW), "bs": _sb(128, U8),
    "ra": _sb(100, I32), "rb": _sb(100, I32), "rc": _sb(100, I32), "rd": _sb(100, I32),
    "ru": _sb(100, U16), "rf": _sb(100, F32), "eg": _sb(960, F32),
    "io2": _sb(1920, F32), "iv": _sb(320, F32), "ew": _sb(2816, F32), "w1": _sb(2560, F32),
    "pe": _sb(1792, F32), "k2": _sb(320, F32), "xc": _sb(256, F32), "xd": _sb(256, F32),
    "c1": _sb(16, F32), "t1": _sb(16, F32), "z1": _sb(16, F32), "z2": _sb(16, F32),
    "cp": _sb(40, F32), "cs": _sb(40, F32), "acs": _sb(24, F32),
    "a0": _sb(16, F32), "a1": _sb(16, F32), "l1": _sb(16, U16), "kg": _sb(256, F32), "ks": _sb(256, F32),
    "x1": _sb(16, F32), "x2": _sb(16, F32), "x3": _sb(16, F32), "x4": _sb(16, F32), "x5": _sb(16, F32), "x6": _sb(16, F32),
    "l2": _sb(16, U16), "fg": _sb(256, F32), "fs": _sb(256, F32), "l3": _sb(16, U16),
    "gt": _sb(512, BF), "yo": _sb(512, BF), "y32": _sb(512, BF), "zl": _sb(512, BF), "xt": _sb(1024, BF), "ys": _sb(256, F32),
    "yq": _sb(128, MXW), "yp": _sb(128, U8), "zq": _sb(128, MXW), "zp": _sb(128, U8),
}
for _b in range(4):
    SCRATCH["dw%d" % _b] = _sb(1792, BF)
    SCRATCH["tm%d" % _b] = _sb(128, F32)
    SCRATCH["xq%d" % _b] = _sb(256, MXW)
    SCRATCH["xs%d" % _b] = _sb(256, U8)
for _n, _d in (("gq", MXW), ("gs", U8), ("rq", MXW), ("rp", U8)):
    SCRATCH[_n] = _sb(384, _d)
for _n, _w, _d in (("ec", 1664, MXW), ("es", 1664, U8), ("ic", 1024, MXW), ("ip", 1024, U8)):
    SCRATCH[_n] = _sb(_w, _d)

SEMAPHORES = ["cv", "cs", "ct", "cg", "dr", "dx", "du", "dv", "dw", "dk", "do", "dp"] + ["ar%d" % t for t in range(3)] + ["lo%d" % t for t in range(3)]


def _tracker(g, T):
    queue = {"v": g.vector, "s": g.scalar, "t": g.tensor, "g": g, "y": g.sync}
    mine = {"v": "cv", "s": "cs", "t": "ct", "g": "cg"}
    count, total = {"v": 0, "s": 0, "t": 0, "g": 0}, {}
    seen = {e: {} for e in queue}
    wrote, read = {}, {}

    def need(e, tok):
        sem, n = tok
        n = total[sem] if n is None else n
        if seen[e].get(sem, 0) < n:
            queue[e].wait_ge(T.sem[sem], n)
            seen[e][sem] = n

    def merge(best, tok):
        sem, n = tok
        n = total[sem] if n is None else n
        best[sem] = max(best.get(sem, 0), n)

    def order(e, rd, wr):
        own, best = mine.get(e), {}
        for k in rd:
            if k in wrote and not (e == "t" and wrote[k][0] == own):
                merge(best, wrote[k])
        for k in wr:
            if k in wrote and not (e == "t" and wrote[k][0] == own):
                merge(best, wrote[k])
            for tok in read.get(k, ()):
                if tok[0] != own:
                    merge(best, tok)
        for sem in best:
            need(e, (sem, best[sem]))

    def note(tok, rd, wr):
        for k in rd:
            read.setdefault(k, []).append(tok)
        for k in wr:
            wrote[k] = tok
            read[k] = []

    def op(e, fn, rd, wr):
        order(e, rd, wr)
        fn(queue[e]).then_inc(T.sem[mine[e]], 1)
        count[e] += 1
        total[mine[e]] = count[e]
        note((mine[e], count[e]), rd, wr)

    def dma(e, out, in_, sem, rd, wr):
        order(e, rd, wr)
        queue[e].dma_start(out, in_).then_inc(T.sem[sem], 16)
        total[sem] = total.get(sem, 0) + 16
        note((sem, None), rd, wr)

    def send(out, in_, sem, lsem, addr, mask, n, rd):
        order("g", rd, ())
        g.remote_dma(out, in_, T.sem[sem], T.sem[lsem], addr[1], addr[0], mask)
        total[lsem] = total.get(lsem, 0) + n
        total[sem] = total.get(sem, 0) + n

    def landed(sem, wr):
        note((sem, None), (), wr)

    def finish():
        for sem in total:
            need("y", (sem, None))

    return op, dma, send, landed, finish


def rank_program(g, core, T, topo):
    rank = T.rank_of(core)
    if rank is None:
        return
    op, dma, send, landed, finish = _tracker(g, T)
    partner = [T.cores[rank ^ m] for m in MASKS]
    emask = topo.mask(core, partner[0])
    for d in partner:
        emask &= topo.mask(core, d)
    engines = bin(emask).count("1")
    COPY, IDENT = F.Copy, F.Identity

    def iota(name, a, b, pattern, base, cm, f32=False, key=None):
        def fn(q):
            if f32:
                return q.iota(T[name][:, a:b], pattern, base, cm, allow_small_or_imprecise_dtypes=True)
            return q.iota(T[name][:, a:b], pattern, base, cm)
        op("g", fn, (), (key or name,))

    def gcopy(out, in_, n, rd, wr):
        op("g", lambda q: q.affine_select(out, in_, [[0, n]], A.is_gt, 0.0, 1, 0), rd, wr)

    def ts(out, in0, s1, op0, rd, wr, s2=None, op1=None):
        if op1 is None:
            op("v", lambda q: q.tensor_scalar(out, in0, s1, None, op0), rd, wr)
        else:
            op("v", lambda q: q.tensor_scalar(out, in0, s1, s2, op0, op1), rd, wr)

    def tt(out, in0, in1, o, rd, wr):
        op("v", lambda q: q.tensor_tensor(out, in0, in1, o), rd, wr)

    def vcopy(out, in_, rd, wr):
        op("v", lambda q: q.tensor_copy(out, in_), rd, wr)

    def act(out, in_, rd, wr, bias=None, scale=None, func=F.Copy):
        if bias is None and scale is None:
            op("s", lambda q: q.activation(out, in_, func), rd, wr)
        elif bias is None:
            op("s", lambda q: q.activation(out, in_, COPY, scale=scale), rd, wr)
        else:
            op("s", lambda q: q.activation(out, in_, IDENT, bias=bias, scale=1.0 if scale is None else scale), rd, wr)

    def quant(out, sc, in_, rd, wr):
        op("v", lambda q: q.quantize_mx(out, sc, in_), rd, wr)

    def mm(bank, n, l, ls, r, rs_, rd, start=True, stop=True):
        out = T.ps[:, 512 * bank:512 * bank + n]
        op("t", lambda q: q.matmul_mx(out, l, ls, r, rs_, start, stop), rd, ("b%d" % bank,))

    def bank(i, n):
        return T.ps[:, 512 * i:512 * i + n]

    def scan(out, d0, d1, rd, wr):
        op("v", lambda q: q.tensor_tensor_scan(out, d0, d1, 0.0, A.mult, A.add), rd, wr)

    def memset(name, val, keys):
        op("v", lambda q: q.memset(T[name][:], val), (), keys)

    dma("s", T.xb[:], T.x[:], "dx", (), ("xb",))
    RL = []
    for d in range(-2, 4):
        c = 20 * (d + 2)
        lo, hi = max(0, -16 * d), min(128, 128 - 16 * d)
        for a, b, f in ((lo, hi, 16 * d), (0, lo, 128 - lo), (hi, 128, -hi)):
            if a < b:
                RL.append("rl%d" % len(RL))
                dma("y", T.rl[a:b, c:c + 20], T.ring[a + f:b + f, :], "dr", (), (RL[-1],))
    dma("s", T.ub[:], T.u[:], "du", (), ("ub",))
    dma("y", T.wq[:].bitcast(dt.uint8), T.wc[:], "dw", (), ("wq",))
    dma("y", T.wp[:], T.ws[:], "dw", (), ("wp",))
    dma("y", T.vb[:], T.v[:], "dv", (), ("vb",))

    iota("pi", 0, 1, [[0, 1]], 0, 1)
    iota("ci", 0, 224, [[32, 7], [0, 2], [1, 16]], 96, 0)
    iota("ci", 224, 416, [[32, 6], [0, 2], [1, 16]], 112, 0, key="ci_")
    iota("io2", 0, 480, [[1, 480]], 0, 0, True)
    iota("li", 0, 60, [[40, 3], [2, 10], [0, 2]], 0, 0)
    iota("ui", 0, 8, [[0, 8]], 0, 16)
    iota("iv", 0, 320, [[-1, 320]], 959, 0, True)
    iota("nn", 0, 256, [[0, 16], [1, 16]], 0, 0, True)
    iota("vi", 0, 40, [[0, 2], [-16, 20]], 319, 0)
    iota("g8", 0, 40, [[0, 5], [1, 8]], 0, 0, True)
    GI = ["gi%d" % i for i in range(10)]
    for i, d in enumerate((0, None, 3, 1, 7, None, 2, None, 3, 1)):
        iota("gi", 8 * i, 8 * i + 8, [[8, 8]] if d is None else [[1, 8]], 9 if d is None else 8 - d, 0, key=GI[i])
    iota("oi", 0, 16, [[16, 16]], 0, 0)
    iota("ew", 2176, 2560, [[1, 384]], 0, 0, True, key="ew_c")
    iota("ii", 0, 128, [[1, 128]], 0, 0)

    memset("et", 0.0, ("et",))
    ts(T.pa[:], T.pi[:], 4, A.arith_shift_right, ("pi",), ("pa",), 1, A.bitwise_and)
    ts(T.pb[:], T.pi[:], 5, A.arith_shift_right, ("pi",), ("pb",))
    ts(T.pk[:], T.pi[:], 15, A.bitwise_and, ("pi",), ("pk",))
    vcopy(T.pf[:], T.pi[:], ("pi",), ("pf",))
    ts(T.cj[:], T.ci[:], 127, A.bitwise_and, ("ci", "ci_"), ("cj",))
    vcopy(T.mo[:], T.pa[:], ("pa",), ("mo",))
    ts(T.me[:], T.pa[:], -1.0, A.mult, ("pa",), ("me",), 1.0, A.add)
    ts(T.fr[:], T.pb[:], -512.0, A.mult, ("pb",), ("fr",), 2560.0, A.add)
    ts(T.et[:, 3:1667:4], T.cj[:], T.pf[:, 0:1], A.is_equal, ("cj", "pf"), ("et",))
    vcopy(T.kf[:], T.pk[:], ("pk",), ("kf",))
    ts(T.ha[:], T.pb[:], -2.0, A.mult, ("pb",), ("ha",))
    ts(T.lu[:], T.li[:], T.mo[:, 0:1], A.add, ("li", "mo"), ("lu",))
    for b in range(4):
        quant(T.ec[:, 416 * b:416 * b + 416], T.es[:, 416 * b:416 * b + 416], T.et[:, 3 - b:1667 - b], ("et",), ("ec%d" % b,))
    ts(T.ra[:], T.rl[:, 20:120], T.me[:, 0:1], A.mult, RL + ["me", "fr"], ("ra",), T.fr[:, 0:1], A.add)
    ts(T.rb[:], T.rl[:, 0:100], T.mo[:, 0:1], A.mult, RL + ["mo"], ("rb",))
    ts(T.s2[:], T.mo[:], 256.0, A.mult, ("mo", "kf"), ("s2",), T.kf[:, 0:1], A.add)
    tt(T.rc[:], T.ra[:], T.rb[:], A.add, ("ra", "rb"), ("rc",))
    ts(T.uj[:], T.ui[:], 112, A.bitwise_and, ("ui",), ("uj",))
    ts(T.rd[:], T.rc[:], 2047, A.bitwise_and, ("rc",), ("rd",))
    vcopy(T.uu[:], T.uj[:], ("uj",), ("uu",))
    vcopy(T.ru[:], T.rd[:], ("rd",), ("ru",))
    vcopy(T.rf[:], T.rd[:], ("rd",), ("rf",))
    quant(T.xq0[:], T.xs0[:], T.xb[:], ("xb",), ("xq0l", "xq0e"))

    act(T.io2[:, 480:960], T.io2[:, 0:480], ("io2",), ("io3",), bias=480.0)
    act(T.w1[:, 1280:1792], T.io2[:, 0:512], ("io2", "io3"), ("po_a",))
    act(T.w1[:, 1792:2048], T.io2[:, 0:256], ("io2",), ("po_b",), bias=1920.0)
    act(T.w1[:, 2048:2560], T.io2[:, 0:512], ("io2", "io3"), ("po_c",))
    act(T.io2[:, 960:1280], T.io2[:, 0:320], ("io2",), ("io4",), bias=960.0)
    act(T.pe[:, 512:1024], T.io2[:, 512:1024], ("io3", "io4"), ("pe",), bias=1280.0)
    act(T.ew[:, 1920:2176], T.io2[:, 512:768], ("io3",), ("ew_a",))
    act(T.ew[:, 2560:2816], T.io2[:, 1024:1280], ("io4",), ("ew_b",))
    act(T.eg[:], T.rf[:].indirect(T.lu[:]), ("rf", "lu"), ("eg",))
    act(T.bt[:], T.io2[:, 0:512], ("io2", "io3"), ("bt0", "bt1"), scale=0.0)
    act(T.ot[:], T.io2[:, 0:512], ("io2", "io3"), ("ot",), bias=1.0, scale=0.0)
    PO = ["po", "po_a", "po_b", "po_c"]

    POOL = {"s": [0, 1, 2, 3], "v": [4, 5, 6], "m": [7]}
    turn = {"s": 0, "v": 0, "m": 0}

    def nextbank(k):
        turn[k] += 1
        return POOL[k][(turn[k] - 1) % len(POOL[k])]

    ALL = [(s, b) for s in range(7) for b in range(4)]
    DWK = [["dw%d_%d%s" % (b, s, h) for s in range(7) for h in "le"] for b in range(4)]

    def slot(e, k, sig, b, halves):
        lo, hi = (0 if "l" in halves else 128), (256 if "e" in halves else 128)
        n = hi - lo
        off = (16 * sig if sig % 2 == 0 else 224 + 16 * (sig - 1)) + 416 * b
        bk = nextbank(e)
        names = ["dw%d_%d%s" % (b, sig, h) for h in halves]
        q, s = T["xq%d" % k], T["xs%d" % k]
        mm(bk, n, T.ec[:, off:off + 128], T.es[:, off:off + 128], q[:, lo:hi], s[:, lo:hi],
           ["ec%d" % b] + ["xq%d%s" % (k, h) for h in halves])

        def copy():
            out = T["dw%d" % b][:, 256 * sig + lo:256 * sig + hi]
            if e == "v":
                vcopy(out, bank(bk, n), ("b%d" % bk,), names)
            else:
                act(out, bank(bk, n), ("b%d" % bk,), names)
        return copy

    def windows(k, halves, todo):
        todo, pending = list(todo), []

        def advance(most=99):
            while todo and most:
                most -= 1
                e, s, b = todo[0]
                if e == "v":
                    if len(pending) >= len(POOL["v"]):
                        return
                    pending.append(slot("v", k, s, b, halves))
                else:
                    slot("s", k, s, b, halves)()
                todo.pop(0)

        def fill():
            if pending:
                pending.pop(0)()
                advance()

        def flush():
            while pending:
                fill()
        return advance, fill, flush

    def deal(nv, skip=0, lead=0):
        if lead:
            return [("v", s, b) for s, b in ALL[:lead]] + deal(nv - lead, lead)
        rest, n = ALL[skip:], len(ALL) - skip
        return [("v" if i * nv // n != (i + 1) * nv // n else "s", s, b) for i, (s, b) in enumerate(rest)]

    def scores(k, h):
        lo = 0 if h == "l" else 128
        bk = nextbank("m")
        mm(bk, 128, T["xq%d" % k][:, lo:lo + 128], T["xs%d" % k][:, lo:lo + 128], T.uq2[:], T.us2[:], ("xq%d%s" % (k, h), "uq2", "us2"))
        i = 0 if h == "l" else 1
        ts(T.bt[:, i:160:4], bank(bk, 40), 0.0, A.is_gt, ("b%d" % bk,), ("bt%d" % i,))

    def counts(t, fill, advance):
        quant(T.bq[:], T.bs[:], T.bt[:], ("bt0", "bt1"), ("bq",))
        bc = nextbank("m")
        mm(bc, 128, T.onc[:], T.ons[:], T.bq[:], T.bs[:], ("on", "bq"))
        advance()
        fill()
        fill()
        fill()
        tt(T.cp[:], bank(bc, 40), T.cm[:], A.mult, ("b%d" % bc, "cm"), ("cp",))
        vcopy(T.acs[:, t:24:3], bank(bc, 8), ("b%d" % bc,), ("acs",))
        scan(T.cs[:], T.r8[:], T.cp[:], ("r8", "cp"), ("cs",))
        fill()

    def chain(h):
        m, w = slice(8 * h, 8 * h + 8), slice(128 * h, 128 * h + 128)
        mk, rs, v, f = T.mk[:, 0:128], T.rs[:, 0:128], T.ks[:, 128 * h + 15:128 * h + 128:16], T.fs[:, 128 * h + 15:128 * h + 128:16]
        k = {n: "%s_%d" % (n, h) for n in ("a0", "a1", "l1", "kg", "ks", "x1", "x2", "x3", "x4", "x5", "x6", "l2", "fg", "fs", "l3")}
        ts(T.a0[:, m], T.t1[:, m], T.cs[:, 7:8], A.min, ("t1", "cs"), (k["a0"],), T.cs[:, 15:16], A.max)
        yield
        tt(T.a1[:, m], T.c1[:, m], T.a0[:, m], A.subtract, ("c1", k["a0"]), (k["a1"],))
        yield
        vcopy(T.l1[:, m], T.a1[:, m], (k["a1"],), (k["l1"],))
        yield
        tt(T.kg[:, w], T.w1[:].indirect(T.l1[:, m]), mk, A.mult, ["w1", "w1_a", "w1_b", k["l1"], "mk"] + PO, (k["kg"],))
        yield
        scan(T.ks[:, w], rs, T.kg[:, w], ("rs", k["kg"]), (k["ks"],))
        yield
        ts(T.x1[:, m], v, 1920.0, A.is_lt, (k["ks"], "cs"), (k["x1"],), T.cs[:, 23:24], A.mult)
        ts(T.x2[:, m], v, 1280.0, A.is_lt, (k["ks"], "cs"), (k["x2"],), T.cs[:, 31:32], A.mult)
        ts(T.x3[:, m], v, 640.0, A.is_lt, (k["ks"], "cs"), (k["x3"],), T.cs[:, 39:40], A.mult)
        yield
        tt(T.x4[:, m], v, T.x1[:, m], A.subtract, (k["ks"], k["x1"]), (k["x4"],))
        tt(T.x5[:, m], T.x2[:, m], T.x3[:, m], A.add, (k["x2"], k["x3"]), (k["x5"],))
        yield
        tt(T.x6[:, m], T.x4[:, m], T.x5[:, m], A.subtract, (k["x4"], k["x5"]), (k["x6"],))
        yield
        vcopy(T.l2[:, m], T.x6[:, m], (k["x6"],), (k["l2"],))
        yield
        tt(T.fg[:, w], T.ew[:].indirect(T.l2[:, m]), mk, A.mult,
           ["ew_a", "ew_b", "ew_c", k["l2"], "mk"] + ["ew%d%s" % (r, c) for r in range(3) for c in "xy"], (k["fg"],))
        yield
        scan(T.fs[:, w], rs, T.fg[:, w], ("rs", k["fg"]), (k["fs"],))
        yield
        vcopy(T.l3[:, m], f, (k["fs"],), (k["l3"],))

    def lists(fill):
        second = chain(1)
        for _ in chain(0):
            next(second, None)
            fill()
        return second

    def gather(buf, half):
        for b in range(4):
            out, src = T[buf][:, b:512:4], T["dw%d" % b][:, 0:1792].indirect(T.l3[:, 8 * half:8 * half + 8])
            (act if b % 2 else vcopy)(out, src, DWK[b] + ["l3_%d" % half], ("%s_%d" % (buf, b),))

    def put_positions(r):
        c = 40 * r
        op("v", lambda q: q.tensor_copy(T.w1[:, 1280:2560].indirect(T.ru[:, c:c + 20]), T.io2[:, 640 * r + 320:640 * r + 640]),
           ("ru", "io2", "io3", "io4"), PO)

    def put_entries(c, src):
        op("v", lambda q: q.tensor_copy(T.pe[:].indirect(T.ru[:, c:c + 20]), src), ("ru", "io2", "io3", "iv"), ("pe",))

    def countmask():
        ts(T.gj[:], T.gi[:], T.ha[:, 0:1], A.add, GI + ["ha"], ("gj",))
        ts(T.mk[:], T.nn[:], T.kf[:, 0:1], A.is_equal, ("nn", "kf"), ("mk",))
        ts(T.gk[:], T.gj[:], 7, A.bitwise_and, ("gj",), ("gk",))
        ts(T.ou[:], T.oi[:], T.s2[:, 0:1], A.add, ("oi", "s2"), ("ou",))
        quant(T.onc[:], T.ons[:], T.ot[:], ("ot",), ("on",))
        ts(T.ge[:], T.gk[:], 0.0, A.is_equal, ("gk",), ("ge",))
        tt(T.xc[:], T.pe[:, 512:1024].indirect(T.ou[:]), T.mk[:], A.mult, ("pe", "ou", "mk"), ("xc",))
        tt(T.cm[:], T.ge[:, 0:40], T.ge[:, 40:80], A.subtract, ("ge",), ("cm",))

    def first():
        for s, b in ALL[:NS_TABLES]:
            slot("s", 0, s, b, "le")()
        put_positions(0)
        quant(T.uq[:], T.us[:], T.ub[:], ("ub",), ("uq",))
        put_entries(20, T.io2[:, 320:640])
        op("v", lambda q: q.tensor_copy(T.uq2[:].bitcast(dt.uint32), T.uq[:].bitcast(dt.uint32).indirect(T.uu[:])), ("uq", "uu"), ("uq2",))
        put_positions(1)
        op("v", lambda q: q.tensor_copy(T.us2[:], T.us[:].indirect(T.uu[:])), ("uq", "uu"), ("us2",))
        ts(T.vu[:], T.vi[:], T.kf[:, 0:1], A.subtract, ("vi", "kf"), ("vu",))
        act(T.w1[:, 320:640], T.w1[:, 1280:2560].indirect(T.ru[:, 20:40]), PO + ["ru"], ("w1_a",))
        dma("y", T.k2[0:96, :], T.w1[32:128, 320:640], "dk", ("w1_a",), ("k2",))
        dma("y", T.k2[96:128, :], T.w1[0:32, 320:640], "dk", ("w1_a",), ("k2_",))
        act(T.rs[:], T.nn[:], ("nn",), ("rs",), func=F.Sign)
        act(T.r8[:], T.g8[:], ("g8",), ("r8",), func=F.Sign)
        for r in range(3):
            op("v", lambda q, r=r: q.transpose(T.ew[:, 640 * r + 320:640 * r + 640], T.eg[:, 320 * r:320 * r + 320]), ("eg",), ("ew%dx" % r,))
        scores(0, "l")
        put_entries(60, T.iv[:])
        for r in range(3):
            gcopy(T.ew[:, 640 * r:640 * r + 320], T.ew[:, 640 * r + 320:640 * r + 640], 320, ("ew%dx" % r,), ("ew%dy" % r,))
        gcopy(T.w1[:, 0:320], T.w1[:, 320:640], 320, ("w1_a",), ("w1",))
        scores(0, "e")
        countmask()
        advance, fill, flush = windows(0, "le", deal(NV_R0, NS_TABLES + NS_MORE))
        for s, b in ALL[NS_TABLES:NS_TABLES + NS_MORE]:
            slot("s", 0, s, b, "le")()
        act(T.w1[:, 640:1280], T.k2[:].indirect(T.vu[:]), ("k2", "k2_", "vu"), ("w1_b",), bias=640.0)
        scan(T.xd[:], T.rs[:], T.xc[:], ("rs", "xc"), ("xd",))
        counts(0, lambda: None, advance)
        fill()
        vcopy(T.c1[:], T.xd[:, 15:256:16], ("xd",), ("c1",))
        fill()
        ts(T.z1[:], T.c1[:], 1280.0, A.is_lt, ("c1",), ("z1",), -4096.0, A.mult)
        ts(T.z2[:], T.c1[:], 640.0, A.is_lt, ("c1",), ("z2",), 8192.0, A.mult)
        fill()
        tt(T.t1[:], T.z1[:], T.z2[:], A.add, ("z1", "z2"), ("t1",))
        second = lists(fill)
        flush()
        return second

    for t in range(3):
        n = t + 1
        if t == 0:
            second = first()
        else:
            advance, fill, flush = windows(t, "l", deal(NV_LATE, 0, 3))
            scores(t, "l")
            advance(3 + NS_COUNT)
            counts(t, fill, advance)
            second = lists(fill)
            flush()
        gather("gt", 0)
        next(second, None)
        w = slice(128 * t, 128 * t + 128)
        quant(T.gq[:, w], T.gs[:, w], T.gt[:], ["gt_%d" % b for b in range(4)], ("gq%d" % t,))
        addr = topo.addr(partner[t])
        send(T.rq[:, w].bitcast(dt.uint8), T.gq[:, w].bitcast(dt.uint8), "ar%d" % t, "lo%d" % t, addr, emask, engines, ("gq%d" % t,))
        send(T.rp[:, w], T.gs[:, w], "ar%d" % t, "lo%d" % t, addr, emask, engines, ("gq%d" % t,))
        landed("ar%d" % t, ("rq%d" % t,))
        gather("yo", 1)
        YO = ["yo_%d" % b for b in range(4)]
        quant(T.yq[:], T.yp[:], T.yo[:], YO, ("yq",))
        ts(T.y32[:], T.yo[:], 32.0, A.mult, YO, ("y32",))
        for b in range(4):
            bk = b
            mm(bk, 128, T.wq[:, 128 * b:128 * b + 128], T.wp[:, 128 * b:128 * b + 128], T.yq[:], T.yp[:], ("wq", "wp", "yq"))
            tt(T["tm%d" % b][:], bank(bk, 128), T.y32[:, b:512:4], A.add, ("b%d" % bk, "y32"), ("tm%d" % b,))
            act(T.xt[:, 512 + b:1024:4], T["tm%d" % b][:], ("tm%d" % b,), ("xe%d" % b,), scale=0.03125)
        if t == 0:
            memset("it", 0.0, ("it",))
        quant(T["xq%d" % n][:, 128:256], T["xs%d" % n][:, 128:256], T.xt[:, 512:1024], ["xe%d" % b for b in range(4)], ("xq%de" % n,))
        if n < 3:
            scores(n, "e")
        if t == 0:
            ts(T.it[:, 3:515:4], T.ii[:], T.pf[:, 0:1], A.is_equal, ("ii", "pf"), ("it",))
            ts(T.it[:, 515:1027:4], T.ii[:], T.pf[:, 0:1], A.is_equal, ("ii", "pf"), ("it",), 32.0, A.mult)
            for b in range(4):
                quant(T.ic[:, 256 * b:256 * b + 256], T.ip[:, 256 * b:256 * b + 256], T.it[:, 3 - b:1027 - b], ("it",), ("ic%d" % b,))
        if n < 3:
            for e, s, b in deal(NV_EARLY):
                slot(e, n, s, b, "e")()
        else:
            mm(7, 128, T.vq[:], T.vs[:], T.xq3[:, 128:256], T.xs3[:, 128:256], ("vq", "xq3e"))
            vcopy(T.ys[:, 128:256], bank(7, 128), ("b7",), ("yse",))
            dma("y", T.y[:, 128:256], T.ys[:, 128:256], "do", ("yse",), ())
            dma("y", T.oc[:, 512:1024], T.xq3[:, 128:256].bitcast(dt.uint8), "do", ("xq3e",), ())
            for i in range(4):
                dma("y", T.osc[4 * i:4 * i + 4, 128:256], T.xs3[32 * i:32 * i + 4, 128:256], "do", ("xq3e",), ())
            dma("y", T.ac[:], T.acs[0:1, 0:24], "do", ("acs",), ())
        rq, rp = T.rq[:, w], T.rp[:, w]
        ub = [0, 4, 1, 5]
        rb = [2, 6, 3, 7]
        for b in range(4):
            mm(ub[b], 128, T.ic[:, 256 * b:256 * b + 128], T.ip[:, 256 * b:256 * b + 128], rq, rp, ("ic%d" % b, "rq%d" % t))
        for b in range(4):
            mm(rb[b], 128, T.ic[:, 256 * b + 128:256 * b + 256], T.ip[:, 256 * b + 128:256 * b + 256], rq, rp, ("ic%d" % b, "rq%d" % t), True, False)
        for b in range(4):
            (vcopy if b % 2 else act)(T.zl[:, b:512:4], bank(ub[b], 128), ("b%d" % ub[b],), ("zl%d" % b,))
        quant(T.zq[:], T.zp[:], T.zl[:], ["zl%d" % b for b in range(4)], ("zq",))
        if t == 1:
            quant(T.vq[:], T.vs[:], T.vb[:], ("vb",), ("vq",))
        for b in range(4):
            mm(rb[b], 128, T.wq[:, 128 * b:128 * b + 128], T.wp[:, 128 * b:128 * b + 128], T.zq[:], T.zp[:], ("wq", "wp", "zq"), False, True)
        for b in range(4):
            if b % 2:
                ts(T.xt[:, b:512:4], bank(rb[b], 128), 0.03125, A.mult, ("b%d" % rb[b],), ("xl%d" % b,))
            else:
                act(T.xt[:, b:512:4], bank(rb[b], 128), ("b%d" % rb[b],), ("xl%d" % b,), scale=0.03125)
        quant(T["xq%d" % n][:, 0:128], T["xs%d" % n][:, 0:128], T.xt[:, 0:512], ["xl%d" % b for b in range(4)], ("xq%dl" % n,))
    mm(7, 128, T.vq[:], T.vs[:], T.xq3[:, 0:128], T.xs3[:, 0:128], ("vq", "xq3l"))
    vcopy(T.ys[:, 0:128], bank(7, 128), ("b7",), ("ysl",))
    dma("s", T.oc[:, 0:512], T.xq3[:, 0:128].bitcast(dt.uint8), "dp", ("xq3l",), ())
    for i in range(4):
        dma("y" if i < 2 else "s", T.osc[4 * i:4 * i + 4, 0:128], T.xs3[32 * i:32 * i + 4, 0:128], "dp", ("xq3l",), ())
    dma("y", T.y[:, 0:128], T.ys[:, 0:128], "dp", ("ysl",), ())
    finish()
